import numpy as np
import ml_dtypes


def mxq(x, axis, fmt="e4m3"):
    dtype, down = {"e4m3": (ml_dtypes.float8_e4m3fn, 7), "e5m2": (ml_dtypes.float8_e5m2, 14)}[fmt]
    v = np.moveaxis(np.asarray(x, np.float32).astype(ml_dtypes.bfloat16).astype(np.float64), axis, -1)
    blocks = v.reshape(v.shape[:-1] + (-1, 32))
    amax = np.abs(blocks).max(-1, keepdims=True)
    byte = np.maximum(np.where(amax > 0, np.frexp(amax)[1] - 1 + 127, 0) - down, 1)
    scale = np.exp2(byte - 127.0)
    codes = (blocks / scale).astype(np.float32).astype(dtype).astype(np.float64)
    return np.moveaxis((codes * scale).reshape(v.shape), -1, axis)


WIDE = False


def mx_kscale(k):
    if not WIDE:
        return np.ones(k)
    levels = np.array([10, -10, 5, -5, 0])
    if k % 512:
        return np.exp2(np.random.permutation(np.resize(levels, k // 32))).repeat(32)
    a = np.empty((k // 512, 16))
    for p in range(k // 512):
        a[p, :8] = np.random.permutation(np.resize(levels, 8))
        for g in range(8):
            far = levels[np.abs(levels - a[p, g]) >= 10]
            a[p, g + 8] = far[np.random.randint(len(far))]
    return np.exp2(a.ravel()).repeat(32)


BF16 = ml_dtypes.bfloat16


def bf(x):
    return np.asarray(x, np.float32).astype(BF16)


def f64(x):
    return np.asarray(x).astype(np.float64)


E2M1 = np.array([0.0, 0.5, 1.0, 1.5, 2.0, 3.0, 4.0, 6.0, -0.0, -0.5, -1.0, -1.5, -2.0, -3.0, -4.0, -6.0])


def pack_weight(w, fmt):
    k, n = w.shape
    w = f64(bf(w)).reshape(k // 32, 32, n)
    amax = np.abs(w).max(1)
    if fmt == "e4m3":
        byte = np.frexp(amax)[1] - 1 + 127 - 7
    else:
        mant, ex = np.frexp(amax / 6.0)
        byte = np.where(mant > 0.5, ex, ex - 1) + 127
    byte = np.clip(np.where(amax > 0, byte, 1), 1, 254)
    scaled = (w * np.exp2(127.0 - byte)[:, None, :]).reshape(k, n).astype(np.float32)
    by_word = np.ascontiguousarray(scaled.reshape(k // 512, 128, 4, n).transpose(0, 1, 3, 2))
    if fmt == "e4m3":
        words = by_word.astype(ml_dtypes.float8_e4m3fn).view(np.uint8)
    else:
        c = by_word.astype(ml_dtypes.float4_e2m1fn).view(np.uint8) & 0xF
        words = c[..., 0::2] | (c[..., 1::2] << 4)
    return np.ascontiguousarray(words), np.ascontiguousarray(byte.astype(np.uint8).reshape(k // 512, 16, n))


def unpack_weight(words, scales, fmt):
    g, p, n, _ = words.shape
    if fmt == "e4m3":
        vals = np.ascontiguousarray(words).view(ml_dtypes.float8_e4m3fn).astype(np.float64)
    else:
        nib = np.empty((g, p, n, 4), np.uint8)
        nib[..., 0::2] = words & 0xF
        nib[..., 1::2] = words >> 4
        vals = E2M1[nib]
    vals = vals * np.repeat(np.exp2(scales.astype(np.float64) - 127.0), 8, axis=1)[..., None]
    return vals.transpose(0, 1, 3, 2).reshape(g * 512, n)
def pack4(w):
    words, scales = pack_weight(w, "e2m1")
    return words.reshape(words.shape[0], 128, -1), scales


def unpack4(words, scales):
    return unpack_weight(words.reshape(words.shape[0], 128, -1, 2), scales, "e2m1")


X, Y, T, D = 1024, 2048, 1024, 512


def draw0():
    a, s, c = mx_kscale(X), mx_kscale(T), mx_kscale(Y)
    u = bf(np.random.standard_normal((X, T)) * a[:, None] * s)
    v = bf(np.random.standard_normal((Y, T)) * c[:, None] / s)
    weight = bf(np.random.uniform(0.5, 1.5, T) / np.sqrt(T))
    rho = bf(np.random.uniform(0.5, 1.5, X))
    model = bf(0.5 * np.random.standard_normal((X, Y)) * a[:, None] * c)
    modes_words, modes_scales = pack4(np.random.standard_normal((Y, D)) / np.sqrt(Y) / c[:, None])
    filt = bf(np.random.standard_normal((D, X)) / np.sqrt(X) / a)
    return {"u": u, "v": v, "weight": weight, "rho": rho, "model": model,
            "modes_words": modes_words, "modes_scales": modes_scales, "filt": filt}


def core(u, v, weight, rho, model, modes_words, modes_scales, filt):
    vw = f64(v) * f64(weight)
    r = mxq(f64(u), 1, "e4m3") @ mxq(vw, 1, "e4m3").T
    stress = r * f64(rho)[:, None] - f64(model)
    coef = mxq(stress, 1, "e4m3") @ unpack4(modes_words, modes_scales)
    resp = mxq(f64(filt), 1, "e4m3") @ mxq(stress, 0, "e4m3")
    return coef, resp


def e4m3fn_bytes(y):
    return np.clip(np.asarray(y, np.float64), -448.0, 448.0).astype(np.float32).astype(ml_dtypes.float8_e4m3fn).view(np.uint8)


def e4m3fn_values(b):
    return np.asarray(b, np.uint8).view(ml_dtypes.float8_e4m3fn).astype(np.float64)


def setup_inputs():
    d = draw0()
    x0 = np.asarray(d['filt']).astype(np.float64)
    s = (np.max(np.abs(x0), axis=(0,), keepdims=True) / 448.0).astype(np.float32)
    out = {}
    for k, v in d.items():
        if k == 'filt':
            out['filt_bytes'] = e4m3fn_bytes(x0 / s.astype(np.float64))
            out['filt_scale'] = s
        else:
            out[k] = v
    return out


def reference(u, v, weight, rho, model, modes_words, modes_scales, filt_bytes, filt_scale):
    return core(u, v, weight, rho, model, modes_words, modes_scales, e4m3fn_values(filt_bytes) * filt_scale.astype(np.float64))

@@ -1,0 +1,342 @@
+from contextlib import ExitStack
+
+import concourse.mybir as mybir
+from concourse.masks import make_identity
+
+X, Y, T, D = 1024, 2048, 1024, 512
+FLOPS = 2 * X * Y * T + 4 * X * Y * D
+
+F32 = mybir.dt.float32
+BF16 = mybir.dt.bfloat16
+I32 = mybir.dt.int32
+U32 = mybir.dt.uint32
+U8 = mybir.dt.uint8
+FP8 = mybir.dt.float8_e4m3fn
+FP8X4 = mybir.dt.float8_e4m3fn_x4
+FP4X4 = mybir.dt.float4_e2m1fn_x4
+MULT = mybir.AluOpType.mult
+SUB = mybir.AluOpType.subtract
+
+P = 128
+PASS = 512
+G, H, KK = X // PASS, Y // PASS, T // PASS
+Q = 4
+
+PROGRAM = """
+BT VT01 VT00 VQ01 UT00 UT01 VQ00 UQ00 UQ01 R001 R000 VM10 R002 R003 ST000 UT10
+VM11 UT11 VT11 UQ11 VT10 ST001 F0 UQ10 SI000 F3 VQ11 R103 VQ10 SI001 R101 R100
+VM20 VM21 R102 R013 R012 R010 F1 F2 R011 LM R110 VT21 VT20 ST011 R113 R111
+SI101 VQ21 R112 VQ20 SI100 ST100 ST101 Y00 FT1 VM30 VM31 R022 FT0 R021 FQ1 X10
+VT30 X00 FQ0 R020 R023 VQ30 ST010 Y01 SI011 Y10 SI010 VT31 R122 P00 SI110 X01
+R121 VQ31 P01 R123 SI111 ST111 ST110 ST020 R120 R033 R032 Y11 R030 R031 SI021 X11
+SI020 R132 R131 R133 R130 ST031 ST021 ST030 Y02 Y03 SI121 P11 P10 SI120 ST131 ST130
+X12 X02 ST121 Y13 ST120 C01 C03 SI031 SI130 SI030 SI131 Y12 P21 C02 C00 X03
+X13 C10 P20 C11 P30 P31 C12 C13
+"""
+ON_V_X = ((0, 2), (0, 3), (1, 1), (1, 3), (2, 1), (2, 2), (2, 3), (3, 0), (3, 1), (3, 2))
+ON_V_Y = ((0, 0), (0, 1), (0, 2), (0, 3), (1, 1))
+
+
+def tile_reynolds_stress_projection_s8_kernel(
+    tc, u, v, weight, rho, model, modes_words, modes_scales, filt_bytes, filt_scale, coef, resp
+):
+    nc = tc.nc
+    with ExitStack() as ctx:
+        keep = ctx.enter_context(tc.tile_pool(name="keep", bufs=1))
+        raw = ctx.enter_context(tc.tile_pool(name="raw", bufs=4))
+        mpool = ctx.enter_context(tc.tile_pool(name="mpool", bufs=3))
+        stage = ctx.enter_context(tc.tile_pool(name="stage", bufs=2))
+        outs = ctx.enter_context(tc.tile_pool(name="outs", bufs=4))
+        psum = ctx.enter_context(tc.psum_pool(name="psum", bufs=8))
+
+        def bank_tile():
+            bank = psum.tile([P, 512], F32, name="bank")
+            return bank
+
+        ident = keep.tile([P, P], F32, name="ident")
+        make_identity(nc, ident[:])
+        w_scales = keep.tile([P, H, D], U8, name="w_scales", align_bytes=64)
+        nc.gpsimd.memset(w_scales[:].rearrange("p h n -> p (h n)").bitcast(I32), 0)
+
+        w4 = keep.tile([P, KK, 2, 2], BF16, name="w4")
+        w8 = keep.tile([P, 8], BF16, name="w8")
+        w8f = keep.tile([P, 8], F32, name="w8f")
+        fs8 = keep.tile([P, 8], F32, name="fs8")
+        rho4 = keep.tile([P, G, Q], BF16, name="rho4")
+        w_b = keep.tile([P, T], BF16, name="w_b")
+        fs_b = keep.tile([P, X], F32, name="fs_b")
+        u_raw, v_raw, m_raw = {}, {}, {}
+        u_view = u.rearrange("(g p t) k -> g p t k", p=P, t=Q)
+        v_view = v.rearrange("(h p q) k -> h p q k", p=P, q=Q)
+        m_view = model.rearrange("(g p t) y -> g p t y", p=P, t=Q)
+
+        def load_rows(view, i, parts):
+            t = raw.tile([P, Q, T], BF16, name="rows")
+            s = Q // parts
+            for j in range(parts):
+                nc.sync.dma_start(out=t[:, j * s : (j + 1) * s, :], in_=view[i, :, j * s : (j + 1) * s, :])
+            return t
+
+        def load_m(g, half, parts):
+            m_raw[g, half] = mpool.tile([P, Q, Y // 2], BF16, name="m_raw")
+            n = Y // 2 // parts
+            return [(g, half, j * n, (j + 1) * n) for j in range(parts)]
+
+        def load_m_part(g, half, lo, hi):
+            base = half * (Y // 2)
+            nc.sync.dma_start(out=m_raw[g, half][:, :, lo:hi], in_=m_view[g, :, :, base + lo : base + hi])
+
+        nc.sync.dma_start(out=w8[:], in_=weight.rearrange("(p c) -> p c", c=8))
+        nc.sync.dma_start(out=fs8[:], in_=filt_scale.rearrange("o (p c) -> p (o c)", c=8))
+        nc.sync.dma_start(out=w4[:].rearrange("p g a b -> p g (a b)"), in_=weight.rearrange("(g p t) -> p g t", p=P, t=Q))
+        v_raw[0] = load_rows(v_view, 0, 4)
+        u_raw[0] = load_rows(u_view, 0, 4)
+        nc.sync.dma_start(out=rho4[:], in_=rho.rearrange("(g p t) -> p g t", p=P, t=Q))
+        m_parts = load_m(0, 0, 2)
+        load_m_part(*m_parts[0])
+        v_raw[1] = load_rows(v_view, 1, 2)
+        u_raw[1] = load_rows(u_view, 1, 2)
+        load_m_part(*m_parts[1])
+        load_m_part(*load_m(1, 0, 1)[0])
+        f_bytes = keep.tile([P, Q, X], U8, name="f_bytes")
+        nc.sync.dma_start(out=f_bytes[:], in_=filt_bytes.rearrange("(p q) k -> p q k", q=Q))
+        v_raw[2] = load_rows(v_view, 2, 2)
+        load_m_part(*load_m(0, 1, 1)[0])
+        v_raw[3] = load_rows(v_view, 3, 2)
+        w_words = keep.tile([P, H, 2 * D], U8, name="w_words", align_bytes=64)
+        nc.sync.dma_start(out=w_words[:], in_=modes_words.rearrange("h p n -> p h n"))
+        for quad in range(4):
+            nc.sync.dma_start(
+                out=w_scales[32 * quad : 32 * quad + 4, :, :].bitcast(I32),
+                in_=modes_scales[:, 4 * quad : 4 * quad + 4, :].rearrange("h r n -> r h n").bitcast(I32),
+            )
+
+        def codes(name, n):
+            c = keep.tile([P, n], U32, name=name, align_bytes=64)
+            s = keep.tile([P, n], U8, name=name + "_s", align_bytes=64)
+            return c, s
+
+        u_c = {(g, kk): codes(f"u_c{g}{kk}", PASS) for g in range(G) for kk in range(KK)}
+        v_c = {(h, kk): codes(f"v_c{h}{kk}", PASS) for h in range(H) for kk in range(KK)}
+        f_c = {g: codes(f"f_c{g}", D) for g in range(G)}
+        x_c = {(g, h): codes(f"x_c{g}{h}", PASS) for g in range(G) for h in range(H)}
+        y_c = {(g, h): codes(f"y_c{g}{h}", PASS) for g in range(G) for h in range(H)}
+
+        def quantize(dst, src, lo=0, hi=PASS):
+            nc.vector.quantize_mx(
+                out=dst[0][:, lo:hi].bitcast(FP8X4),
+                scales=dst[1][:, lo:hi],
+                in_=src[:].rearrange("p n j -> p (n j)")[:, 4 * lo : 4 * hi],
+            )
+
+        def mx(out, a, a_cols, b, b_cols, start, stop):
+            nc.tensor.matmul_mx(
+                out=out, lhsT=a[0][:, a_cols].bitcast(FP8X4), lhsT_scale=a[1][:, a_cols],
+                rhs=b[0][:, b_cols].bitcast(FP8X4), rhs_scale=b[1][:, b_cols], start=start, stop=stop,
+            )
+
+        def copy_out(eng, out, in_):
+            if eng == "v":
+                nc.vector.tensor_copy(out=out, in_=in_)
+            else:
+                nc.scalar.copy(out=out, in_=in_)
+
+        def words_out(dst, b, bank, eng):
+            o = dst[:, 256 * b : 256 * b + 256, :].rearrange("p r j -> p (r j)").bitcast(F32).rearrange("p (r w) -> p r w", w=2)
+            copy_out(eng, o, bank[:].rearrange("p (w r) -> p r w", w=2))
+
+        def turn(bank, src, b, kk):
+            for w in range(2):
+                for e in range(2):
+                    words = src[:, 2 * b + e, :].bitcast(F32)
+                    at = 256 * w + 128 * e
+                    nc.tensor.transpose(bank[:, at : at + P], words[:, 256 * kk + w : 256 * kk + 256 : 2], ident[:])
+
+        def turn_sorted(bank, src, b, kk):
+            for w in range(2):
+                for e in range(2):
+                    words = src[:, 2 * b + e, :].bitcast(F32)
+                    at = 256 * w + 128 * e
+                    lo = 256 * w + 128 * kk
+                    nc.tensor.transpose(bank[:, at : at + P], words[:, lo : lo + P], ident[:])
+
+        def load_last():
+            load_m_part(*load_m(1, 1, 1)[0])
+
+        def broadcast():
+            nc.vector.tensor_copy(out=w8f[:], in_=w8[:])
+            for src, dst in ((w8f, w_b), (fs8, fs_b)):
+                for j in range(2):
+                    bank = bank_tile()
+                    for c in range(4):
+                        nc.tensor.transpose(
+                            bank[:, P * c : P * c + P], src[:, 4 * j + c : 4 * j + c + 1].to_broadcast([P, P]), ident[:]
+                        )
+                    nc.scalar.copy(
+                        out=dst[:].rearrange("p (w a j e) -> p j w a e", w=2, a=P, j=2)[:, j, :, :, :],
+                        in_=bank[:].rearrange("p (w e a) -> p w a e", w=2, e=2),
+                    )
+
+        st = {}
+
+        def u_turn(g, kk):
+            st["u", g, kk] = stage.tile([P, PASS, 4], BF16, name="u_st", align_bytes=64)
+            for b in range(2):
+                bank = bank_tile()
+                turn(bank, u_raw[g], b, kk)
+                words_out(st["u", g, kk], b, bank, "s")
+
+        def u_quant(g, b):
+            for kk in range(KK):
+                quantize(u_c[g, kk], st["u", g, kk], 256 * b, 256 * b + 256)
+
+        def v_turn0(h, kk):
+            st["v", h, kk] = stage.tile([P, PASS, 4], BF16, name="v_st", align_bytes=64)
+            for b in range(2):
+                bank = bank_tile()
+                turn(bank, v_raw[h], b, kk)
+                nc.vector.tensor_tensor(
+                    out=st["v", h, kk][:, 256 * b : 256 * b + 256, :].rearrange("p r (w e) -> p r w e", w=2),
+                    in0=bank[:].bitcast(BF16).rearrange("p (w r e) -> p r w e", w=2, e=2),
+                    in1=w4[:, kk : kk + 1, :, :].to_broadcast([P, 256, 2, 2]),
+                    op=MULT,
+                )
+
+        v_m = {}
+
+        def sorted_words(ap):
+            return ap.rearrange("p (k w e) -> p w k e", w=2, e=2)
+
+        def in_order(ap):
+            return ap.rearrange("p (w k e) -> p w k e", w=2, e=2)
+
+        def v_mult(h, b):
+            if h not in v_m:
+                v_m[h] = stage.tile([P, Q, T], BF16, name="v_m")
+            for q in (2 * b, 2 * b + 1):
+                nc.vector.tensor_tensor(
+                    out=in_order(v_m[h][:, q, :]), in0=sorted_words(v_raw[h][:, q, :]), in1=in_order(w_b[:]), op=MULT
+                )
+
+        def v_turn(h, kk):
+            if h == 0:
+                v_turn0(h, kk)
+                return
+            st["v", h, kk] = stage.tile([P, PASS, 4], BF16, name="v_st", align_bytes=64)
+            for b in range(2):
+                bank = bank_tile()
+                turn_sorted(bank, v_m[h], b, kk)
+                words_out(st["v", h, kk], b, bank, "s")
+
+        def v_quant(h, kk):
+            quantize(v_c[h, kk], st["v", h, kk])
+
+        s_t, x_st, y_st = {}, {}, {}
+
+        def stress(g, h, t):
+            if (g, h) not in s_t:
+                s_t[g, h] = stage.tile([P, Q, PASS], BF16, name="s_t", align_bytes=64, bufs=3)
+            bank = bank_tile()
+            for kk in range(KK):
+                mx(bank[:], u_c[g, kk], slice(P * t, P * t + P), v_c[h, kk], slice(0, PASS), kk == 0, kk == KK - 1)
+            m = m_raw[g, h // 2][:, t, PASS * (h % 2) : PASS * (h % 2) + PASS]
+            for w in range(2):
+                nc.vector.scalar_tensor_tensor(
+                    out=s_t[g, h][:, t, 256 * w : 256 * w + 256].rearrange("p (c e) -> p c e", e=2),
+                    in0=bank[:, 256 * w : 256 * w + 256].rearrange("p (e c) -> p c e", e=2),
+                    scalar=rho4[:, g, t : t + 1],
+                    in1=m.rearrange("p (c w e) -> p w c e", w=2, e=2)[:, w, :, :],
+                    op0=MULT,
+                    op1=SUB,
+                )
+
+        def s_turn(g, h, b):
+            if (g, h) not in y_st:
+                y_st[g, h] = stage.tile([P, PASS, 4], BF16, name="y_st", align_bytes=64)
+            bank = bank_tile()
+            for w in range(2):
+                for e in range(2):
+                    words = s_t[g, h][:, 2 * b + e, :].bitcast(F32)
+                    at = 256 * w + 128 * e
+                    nc.tensor.transpose(bank[:, at : at + P], words[:, P * w : P * w + P], ident[:])
+            words_out(y_st[g, h], b, bank, "s")
+
+        def s_inter(g, h, half):
+            if (g, h) not in x_st:
+                x_st[g, h] = stage.tile([P, PASS, Q], BF16, name="x_st", align_bytes=64)
+            n = slice(256 * half, 256 * half + 256)
+            nc.scalar.copy(
+                out=x_st[g, h][:, n, :].rearrange("p (c i) t -> p c t i", i=4),
+                in_=s_t[g, h][:, :, n].rearrange("p t (c i) -> p c t i", i=4),
+            )
+
+        def x_quant(g, h):
+            quantize(x_c[g, h], x_st[g, h])
+
+        def y_quant(g, h):
+            quantize(y_c[g, h], y_st[g, h])
+
+        f_bf = keep.tile([P, Q, X], BF16, name="f_bf")
+
+        def f_scale(q):
+            f_cast = stage.tile([P, X], BF16, name="f_cast")
+            nc.scalar.copy(out=f_cast[:], in_=f_bytes[:, q, :].bitcast(FP8))
+            nc.gpsimd.tensor_tensor(
+                out=in_order(f_bf[:, q, :]), in0=sorted_words(f_cast[:]), in1=in_order(fs_b[:]), op=MULT
+            )
+
+        def f_turn(g):
+            st["f", g] = stage.tile([P, PASS, 4], BF16, name="u_st", align_bytes=64)
+            for b in range(2):
+                bank = bank_tile()
+                turn_sorted(bank, f_bf, b, g)
+                words_out(st["f", g], b, bank, "s")
+
+        def f_quant(g):
+            quantize(f_c[g], st["f", g])
+
+        resp_view = resp.rearrange("(m q) y -> q m y", q=Q)
+        coef_view = coef.rearrange("(g m t) d -> g t m d", m=P, t=Q)
+
+        def project_x(h, b):
+            for q in (2 * b, 2 * b + 1):
+                bank = bank_tile()
+                for g in range(G):
+                    mx(bank[:], f_c[g], slice(P * q, P * q + P), x_c[g, h], slice(0, PASS), g == 0, g == G - 1)
+                o = outs.tile([P, PASS], F32, name="o_sb")
+                copy_out(
+                    "v" if (h, q) in ON_V_X else "s",
+                    o[:].rearrange("p (c w e) -> p c w e", w=2, e=2),
+                    bank[:].rearrange("p (w c e) -> p c w e", w=2, e=2),
+                )
+                nc.sync.dma_start(out=resp_view[q, :, PASS * h : PASS * h + PASS], in_=o[:])
+
+        def project_y(g, t):
+            bank = bank_tile()
+            for h in range(H):
+                nc.tensor.matmul_mx(
+                    out=bank[:],
+                    lhsT=y_c[g, h][0][:, P * t : P * t + P].bitcast(FP8X4),
+                    lhsT_scale=y_c[g, h][1][:, P * t : P * t + P],
+                    rhs=w_words[:, h, :].bitcast(FP4X4),
+                    rhs_scale=w_scales[:, h, :],
+                    start=h == 0,
+                    stop=h == H - 1,
+                )
+            o = outs.tile([P, D], F32, name="o_sb")
+            copy_out("v" if (g, t) in ON_V_Y else "s", o[:], bank[:])
+            nc.sync.dma_start(out=coef_view[g, t], in_=o[:])
+
+        units = {
+            "BT": broadcast, "UT": u_turn, "UQ": u_quant, "VM": v_mult, "VT": v_turn, "VQ": v_quant,
+            "R": stress, "ST": s_turn, "SI": s_inter, "X": x_quant, "Y": y_quant,
+            "F": f_scale, "FT": f_turn, "FQ": f_quant, "P": project_x, "C": project_y, "LM": load_last,
+        }
+        with tc.manual_schedule():
+            for word in PROGRAM.split():
+                n = len(word)
+                cut = n
+                for i in range(n):
+                    if word[i] in "01234567" and cut == n:
+                        cut = i
+                units[word[:cut]](*[int(c) for c in word[cut:]])

@@ -23,18 +23,18 @@ G, H, KK = X // PASS, Y // PASS, T // PASS
 Q = 4
 
 PROGRAM = """
-BT VT01 VT00 VQ01 UT00 UT01 VQ00 UQ00 UQ01 R001 R000 VM10 R002 R003 ST000 UT10
-VM11 UT11 VT11 UQ11 VT10 ST001 F0 UQ10 SI000 F3 VQ11 R103 VQ10 SI001 R101 R100
-VM20 VM21 R102 R013 R012 R010 F1 F2 R011 LM R110 VT21 VT20 ST011 R113 R111
-SI101 VQ21 R112 VQ20 SI100 ST100 ST101 Y00 FT1 VM30 VM31 R022 FT0 R021 FQ1 X10
-VT30 X00 FQ0 R020 R023 VQ30 ST010 Y01 SI011 Y10 SI010 VT31 R122 P00 SI110 X01
-R121 VQ31 P01 R123 SI111 ST111 ST110 ST020 R120 R033 R032 Y11 R030 R031 SI021 X11
-SI020 R132 R131 R133 R130 ST031 ST021 ST030 Y02 Y03 SI121 P11 P10 SI120 ST131 ST130
-X12 X02 ST121 Y13 ST120 C01 C03 SI031 SI130 SI030 SI131 Y12 P21 C02 C00 X03
-X13 C10 P20 C11 P30 P31 C12 C13
+BT VT01 VT00 UT00 UT01 VQ00 UT10 VQ01 UT11 UQ00 UQ01 VM11 UQ10 R002 F0 UQ11
+VM10 R003 F2 R000 VM20 R001 VM21 VT11 VQ11 VT10 VQ10 F1 R103 ST001 R102 R100
+F3 R101 VT20 R012 R011 VQ20 ST101 VM31 VT21 ST000 R010 SI001 VM30 ST100 R013 SI000
+SI101 VQ21 R113 R112 R111 R110 SI100 FT1 X00 FT0 Y10 R022 Y00 R021 X10 FQ0
+SI010 VT30 R023 SI011 R020 VT31 FQ1 R121 R122 VQ30 ST010 ST011 R120 VQ31 R123 SI110
+P00 SI111 ST110 Y01 ST111 X11 ST021 ST020 X01 SI021 R033 SI020 R030 R031 R032 P01
+Y11 R133 R130 R131 P11 R132 ST031 ST030 Y02 ST120 ST121 Y03 X02 P10 ST130 ST131
+SI121 C00 Y13 Y12 C01 SI120 C03 X12 SI130 C02 SI031 C10 P20 SI131 SI030 C12
+C11 X13 P21 X03 C13 P31 P30
 """
-ON_V_X = ((0, 2), (0, 3), (1, 1), (1, 3), (2, 1), (2, 2), (2, 3), (3, 0), (3, 1), (3, 2))
-ON_V_Y = ((0, 0), (0, 1), (0, 2), (0, 3), (1, 1))
+ON_V_X = ((0, 0), (0, 1), (1, 0), (1, 1), (2, 0), (2, 1), (3, 1))
+ON_V_Y = ((0, 0), (0, 1), (0, 2), (0, 3), (1, 0), (1, 2))
 
 
 def tile_reynolds_stress_projection_s8_kernel(
@@ -44,7 +44,6 @@ def tile_reynolds_stress_projection_s8_kernel(
     with ExitStack() as ctx:
         keep = ctx.enter_context(tc.tile_pool(name="keep", bufs=1))
         raw = ctx.enter_context(tc.tile_pool(name="raw", bufs=4))
-        mpool = ctx.enter_context(tc.tile_pool(name="mpool", bufs=3))
         stage = ctx.enter_context(tc.tile_pool(name="stage", bufs=2))
         outs = ctx.enter_context(tc.tile_pool(name="outs", bufs=4))
         psum = ctx.enter_context(tc.psum_pool(name="psum", bufs=8))
@@ -70,46 +69,61 @@ def tile_reynolds_stress_projection_s8_kernel(
         v_view = v.rearrange("(h p q) k -> h p q k", p=P, q=Q)
         m_view = model.rearrange("(g p t) y -> g p t y", p=P, t=Q)
 
-        def load_rows(view, i, parts):
-            t = raw.tile([P, Q, T], BF16, name="rows")
-            s = Q // parts
-            for j in range(parts):
-                nc.sync.dma_start(out=t[:, j * s : (j + 1) * s, :], in_=view[i, :, j * s : (j + 1) * s, :])
-            return t
-
-        def load_m(g, half, parts):
-            m_raw[g, half] = mpool.tile([P, Q, Y // 2], BF16, name="m_raw")
-            n = Y // 2 // parts
-            return [(g, half, j * n, (j + 1) * n) for j in range(parts)]
-
-        def load_m_part(g, half, lo, hi):
-            base = half * (Y // 2)
-            nc.sync.dma_start(out=m_raw[g, half][:, :, lo:hi], in_=m_view[g, :, :, base + lo : base + hi])
-
+        w_words = keep.tile([P, H, 2 * D], U8, name="w_words", align_bytes=64)
         nc.sync.dma_start(out=w8[:], in_=weight.rearrange("(p c) -> p c", c=8))
         nc.sync.dma_start(out=fs8[:], in_=filt_scale.rearrange("o (p c) -> p (o c)", c=8))
         nc.sync.dma_start(out=w4[:].rearrange("p g a b -> p g (a b)"), in_=weight.rearrange("(g p t) -> p g t", p=P, t=Q))
-        v_raw[0] = load_rows(v_view, 0, 4)
-        u_raw[0] = load_rows(u_view, 0, 4)
+        v_raw[0] = raw.tile([P, Q, T], BF16, name="rows")
+        nc.sync.dma_start(out=v_raw[0][:, 0:1, :], in_=v_view[0, :, 0:1, :])
+        nc.sync.dma_start(out=v_raw[0][:, 1:2, :], in_=v_view[0, :, 1:2, :])
+        nc.sync.dma_start(out=v_raw[0][:, 2:3, :], in_=v_view[0, :, 2:3, :])
+        nc.sync.dma_start(out=v_raw[0][:, 3:4, :], in_=v_view[0, :, 3:4, :])
+        u_raw[0] = raw.tile([P, Q, T], BF16, name="rows")
+        nc.sync.dma_start(out=u_raw[0][:, 0:1, :], in_=u_view[0, :, 0:1, :])
+        nc.sync.dma_start(out=u_raw[0][:, 1:2, :], in_=u_view[0, :, 1:2, :])
+        nc.sync.dma_start(out=u_raw[0][:, 2:3, :], in_=u_view[0, :, 2:3, :])
+        nc.sync.dma_start(out=u_raw[0][:, 3:4, :], in_=u_view[0, :, 3:4, :])
+        u_raw[1] = raw.tile([P, Q, T], BF16, name="rows")
+        nc.sync.dma_start(out=u_raw[1][:, 0:2, :], in_=u_view[1, :, 0:2, :])
+        nc.sync.dma_start(out=u_raw[1][:, 2:4, :], in_=u_view[1, :, 2:4, :])
+        v_raw[1] = raw.tile([P, Q, T], BF16, name="rows")
+        nc.sync.dma_start(out=v_raw[1][:, 2:4, :], in_=v_view[1, :, 2:4, :])
+        m_raw[0, 0] = keep.tile([P, Q, Y // 2], BF16, name="m_raw00")
+        nc.sync.dma_start(out=m_raw[0, 0][:, :, 0:512], in_=m_view[0, :, :, 0:512])
+        nc.sync.dma_start(out=v_raw[1][:, 0:2, :], in_=v_view[1, :, 0:2, :])
         nc.sync.dma_start(out=rho4[:], in_=rho.rearrange("(g p t) -> p g t", p=P, t=Q))
-        m_parts = load_m(0, 0, 2)
-        load_m_part(*m_parts[0])
-        v_raw[1] = load_rows(v_view, 1, 2)
-        u_raw[1] = load_rows(u_view, 1, 2)
-        load_m_part(*m_parts[1])
-        load_m_part(*load_m(1, 0, 1)[0])
         f_bytes = keep.tile([P, Q, X], U8, name="f_bytes")
         nc.sync.dma_start(out=f_bytes[:], in_=filt_bytes.rearrange("(p q) k -> p q k", q=Q))
-        v_raw[2] = load_rows(v_view, 2, 2)
-        load_m_part(*load_m(0, 1, 1)[0])
-        v_raw[3] = load_rows(v_view, 3, 2)
-        w_words = keep.tile([P, H, 2 * D], U8, name="w_words", align_bytes=64)
+        v_raw[2] = raw.tile([P, Q, T], BF16, name="rows")
+        nc.sync.dma_start(out=v_raw[2][:, 0:2, :], in_=v_view[2, :, 0:2, :])
+        nc.sync.dma_start(out=v_raw[2][:, 2:4, :], in_=v_view[2, :, 2:4, :])
+        m_raw[1, 0] = keep.tile([P, Q, Y // 2], BF16, name="m_raw10")
+        nc.sync.dma_start(out=m_raw[1, 0][:, :, 0:1024], in_=m_view[1, :, :, 0:1024])
+        nc.sync.dma_start(out=m_raw[0, 0][:, :, 512:1024], in_=m_view[0, :, :, 512:1024])
+        v_raw[3] = raw.tile([P, Q, T], BF16, name="rows")
+        nc.sync.dma_start(out=v_raw[3][:, 0:2, :], in_=v_view[3, :, 0:2, :])
+        nc.sync.dma_start(out=v_raw[3][:, 2:4, :], in_=v_view[3, :, 2:4, :])
+        m_raw[0, 1] = keep.tile([P, Q, Y // 2], BF16, name="m_raw01")
+        nc.sync.dma_start(out=m_raw[0, 1][:, :, 0:1024], in_=m_view[0, :, :, 1024:2048])
+        m_raw[1, 1] = keep.tile([P, Q, Y // 2], BF16, name="m_raw11")
+        nc.sync.dma_start(out=m_raw[1, 1][:, :, 0:1024], in_=m_view[1, :, :, 1024:2048])
+        nc.sync.dma_start(
+            out=w_scales[0 : 4, :, :].bitcast(I32),
+            in_=modes_scales[:, 0 : 4, :].rearrange("h r n -> r h n").bitcast(I32),
+        )
+        nc.sync.dma_start(
+            out=w_scales[32 : 36, :, :].bitcast(I32),
+            in_=modes_scales[:, 4 : 8, :].rearrange("h r n -> r h n").bitcast(I32),
+        )
         nc.sync.dma_start(out=w_words[:], in_=modes_words.rearrange("h p n -> p h n"))
-        for quad in range(4):
-            nc.sync.dma_start(
-                out=w_scales[32 * quad : 32 * quad + 4, :, :].bitcast(I32),
-                in_=modes_scales[:, 4 * quad : 4 * quad + 4, :].rearrange("h r n -> r h n").bitcast(I32),
-            )
+        nc.sync.dma_start(
+            out=w_scales[64 : 68, :, :].bitcast(I32),
+            in_=modes_scales[:, 8 : 12, :].rearrange("h r n -> r h n").bitcast(I32),
+        )
+        nc.sync.dma_start(
+            out=w_scales[96 : 100, :, :].bitcast(I32),
+            in_=modes_scales[:, 12 : 16, :].rearrange("h r n -> r h n").bitcast(I32),
+        )
 
         def codes(name, n):
             c = keep.tile([P, n], U32, name=name, align_bytes=64)
@@ -159,9 +173,6 @@ def tile_reynolds_stress_projection_s8_kernel(
                     at = 256 * w + 128 * e
                     lo = 256 * w + 128 * kk
                     nc.tensor.transpose(bank[:, at : at + P], words[:, lo : lo + P], ident[:])
-
-        def load_last():
-            load_m_part(*load_m(1, 1, 1)[0])
 
         def broadcast():
             nc.vector.tensor_copy(out=w8f[:], in_=w8[:])
@@ -330,7 +341,7 @@ def tile_reynolds_stress_projection_s8_kernel(
         units = {
             "BT": broadcast, "UT": u_turn, "UQ": u_quant, "VM": v_mult, "VT": v_turn, "VQ": v_quant,
             "R": stress, "ST": s_turn, "SI": s_inter, "X": x_quant, "Y": y_quant,
-            "F": f_scale, "FT": f_turn, "FQ": f_quant, "P": project_x, "C": project_y, "LM": load_last,
+            "F": f_scale, "FT": f_turn, "FQ": f_quant, "P": project_x, "C": project_y,
         }
         with tc.manual_schedule():
             for word in PROGRAM.split():

@@ -23,18 +23,18 @@ G, H, KK = X // PASS, Y // PASS, T // PASS
 Q = 4
 
 PROGRAM = """
-BT VT01 VT00 UT00 UT01 VQ00 UT10 VQ01 UT11 UQ00 UQ01 VM11 UQ10 R002 F0 UQ11
-VM10 R003 F2 R000 VM20 R001 VM21 VT11 VQ11 VT10 VQ10 F1 R103 ST001 R102 R100
-F3 R101 VT20 R012 R011 VQ20 ST101 VM31 VT21 ST000 R010 SI001 VM30 ST100 R013 SI000
-SI101 VQ21 R113 R112 R111 R110 SI100 FT1 X00 FT0 Y10 R022 Y00 R021 X10 FQ0
-SI010 VT30 R023 SI011 R020 VT31 FQ1 R121 R122 VQ30 ST010 ST011 R120 VQ31 R123 SI110
-P00 SI111 ST110 Y01 ST111 X11 ST021 ST020 X01 SI021 R033 SI020 R030 R031 R032 P01
-Y11 R133 R130 R131 P11 R132 ST031 ST030 Y02 ST120 ST121 Y03 X02 P10 ST130 ST131
-SI121 C00 Y13 Y12 C01 SI120 C03 X12 SI130 C02 SI031 C10 P20 SI131 SI030 C12
-C11 X13 P21 X03 C13 P31 P30
+BT VT01 VT00 VQ00 UT00 VQ01 UT01 UQ01 UT10 F3 UQ00 R003 R000 R002 R001 F1
+UQ10 UT11 VT10 UQ11 VT11 F2 ST001 VQ10 ST000 VQ11 R100 R101 F0 R102 R103 R011
+SI001 R012 R010 SI000 SI100 R013 SI101 R113 ST100 Y00 R110 FT0 X10 FT1 X00 FQ0
+ST010 ST011 SI011 VT20 SI010 FQ1 ST101 VQ20 VT21 Y01 R111 VQ21 P01 R112 P00 Y10
+VT31 SI111 R020 R021 R023 R022 VT30 VQ31 SI110 ST020 VQ30 X01 ST110 X11 ST111 ST021
+R122 R121 R120 SI021 R123 R132 SI020 R032 P11 R033 R031 SI121 R030 Y02 SI120 R130
+R133 P10 ST031 ST030 ST121 R131 ST120 ST131 ST130 SI131 Y03 Y11 X02 SI130 Y12 SI031
+SI030 C03 X12 C01 Y13 C02 C00 P20 C13 P21 X13 X03 C12 P31 P30 C10
+C11
 """
-ON_V_X = ((0, 0), (0, 1), (1, 0), (1, 1), (2, 0), (2, 1), (3, 1))
-ON_V_Y = ((0, 0), (0, 1), (0, 2), (0, 3), (1, 0), (1, 2))
+ON_V_X = ((2, 0), (2, 1), (3, 0), (3, 2), (3, 3))
+ON_V_Y = ((0, 0), (0, 1), (0, 2), (0, 3), (1, 2))
 
 
 def tile_reynolds_stress_projection_s8_kernel(
@@ -58,11 +58,8 @@ def tile_reynolds_stress_projection_s8_kernel(
         nc.gpsimd.memset(w_scales[:].rearrange("p h n -> p (h n)").bitcast(I32), 0)
 
         w4 = keep.tile([P, KK, 2, 2], BF16, name="w4")
-        w8 = keep.tile([P, 8], BF16, name="w8")
-        w8f = keep.tile([P, 8], F32, name="w8f")
         fs8 = keep.tile([P, 8], F32, name="fs8")
         rho4 = keep.tile([P, G, Q], BF16, name="rho4")
-        w_b = keep.tile([P, T], BF16, name="w_b")
         fs_b = keep.tile([P, X], F32, name="fs_b")
         u_raw, v_raw, m_raw = {}, {}, {}
         u_view = u.rearrange("(g p t) k -> g p t k", p=P, t=Q)
@@ -70,7 +67,6 @@ def tile_reynolds_stress_projection_s8_kernel(
         m_view = model.rearrange("(g p t) y -> g p t y", p=P, t=Q)
 
         w_words = keep.tile([P, H, 2 * D], U8, name="w_words", align_bytes=64)
-        nc.sync.dma_start(out=w8[:], in_=weight.rearrange("(p c) -> p c", c=8))
         nc.sync.dma_start(out=fs8[:], in_=filt_scale.rearrange("o (p c) -> p (o c)", c=8))
         nc.sync.dma_start(out=w4[:].rearrange("p g a b -> p g (a b)"), in_=weight.rearrange("(g p t) -> p g t", p=P, t=Q))
         v_raw[0] = raw.tile([P, Q, T], BF16, name="rows")
@@ -86,27 +82,18 @@ def tile_reynolds_stress_projection_s8_kernel(
         u_raw[1] = raw.tile([P, Q, T], BF16, name="rows")
         nc.sync.dma_start(out=u_raw[1][:, 0:2, :], in_=u_view[1, :, 0:2, :])
         nc.sync.dma_start(out=u_raw[1][:, 2:4, :], in_=u_view[1, :, 2:4, :])
-        v_raw[1] = raw.tile([P, Q, T], BF16, name="rows")
-        nc.sync.dma_start(out=v_raw[1][:, 2:4, :], in_=v_view[1, :, 2:4, :])
         m_raw[0, 0] = keep.tile([P, Q, Y // 2], BF16, name="m_raw00")
         nc.sync.dma_start(out=m_raw[0, 0][:, :, 0:512], in_=m_view[0, :, :, 0:512])
-        nc.sync.dma_start(out=v_raw[1][:, 0:2, :], in_=v_view[1, :, 0:2, :])
-        nc.sync.dma_start(out=rho4[:], in_=rho.rearrange("(g p t) -> p g t", p=P, t=Q))
         f_bytes = keep.tile([P, Q, X], U8, name="f_bytes")
         nc.sync.dma_start(out=f_bytes[:], in_=filt_bytes.rearrange("(p q) k -> p q k", q=Q))
+        v_raw[1] = raw.tile([P, Q, T], BF16, name="rows")
+        nc.sync.dma_start(out=v_raw[1][:, 0:2, :], in_=v_view[1, :, 0:2, :])
+        nc.sync.dma_start(out=v_raw[1][:, 2:4, :], in_=v_view[1, :, 2:4, :])
+        nc.sync.dma_start(out=rho4[:], in_=rho.rearrange("(g p t) -> p g t", p=P, t=Q))
         v_raw[2] = raw.tile([P, Q, T], BF16, name="rows")
         nc.sync.dma_start(out=v_raw[2][:, 0:2, :], in_=v_view[2, :, 0:2, :])
-        nc.sync.dma_start(out=v_raw[2][:, 2:4, :], in_=v_view[2, :, 2:4, :])
         m_raw[1, 0] = keep.tile([P, Q, Y // 2], BF16, name="m_raw10")
         nc.sync.dma_start(out=m_raw[1, 0][:, :, 0:1024], in_=m_view[1, :, :, 0:1024])
-        nc.sync.dma_start(out=m_raw[0, 0][:, :, 512:1024], in_=m_view[0, :, :, 512:1024])
-        v_raw[3] = raw.tile([P, Q, T], BF16, name="rows")
-        nc.sync.dma_start(out=v_raw[3][:, 0:2, :], in_=v_view[3, :, 0:2, :])
-        nc.sync.dma_start(out=v_raw[3][:, 2:4, :], in_=v_view[3, :, 2:4, :])
-        m_raw[0, 1] = keep.tile([P, Q, Y // 2], BF16, name="m_raw01")
-        nc.sync.dma_start(out=m_raw[0, 1][:, :, 0:1024], in_=m_view[0, :, :, 1024:2048])
-        m_raw[1, 1] = keep.tile([P, Q, Y // 2], BF16, name="m_raw11")
-        nc.sync.dma_start(out=m_raw[1, 1][:, :, 0:1024], in_=m_view[1, :, :, 1024:2048])
         nc.sync.dma_start(
             out=w_scales[0 : 4, :, :].bitcast(I32),
             in_=modes_scales[:, 0 : 4, :].rearrange("h r n -> r h n").bitcast(I32),
@@ -115,15 +102,24 @@ def tile_reynolds_stress_projection_s8_kernel(
             out=w_scales[32 : 36, :, :].bitcast(I32),
             in_=modes_scales[:, 4 : 8, :].rearrange("h r n -> r h n").bitcast(I32),
         )
-        nc.sync.dma_start(out=w_words[:], in_=modes_words.rearrange("h p n -> p h n"))
+        nc.sync.dma_start(out=m_raw[0, 0][:, :, 512:1024], in_=m_view[0, :, :, 512:1024])
+        m_raw[0, 1] = keep.tile([P, Q, Y // 2], BF16, name="m_raw01")
+        nc.sync.dma_start(out=m_raw[0, 1][:, :, 0:1024], in_=m_view[0, :, :, 1024:2048])
+        v_raw[3] = raw.tile([P, Q, T], BF16, name="rows")
+        nc.sync.dma_start(out=v_raw[3][:, 0:2, :], in_=v_view[3, :, 0:2, :])
+        nc.sync.dma_start(out=v_raw[2][:, 2:4, :], in_=v_view[2, :, 2:4, :])
+        m_raw[1, 1] = keep.tile([P, Q, Y // 2], BF16, name="m_raw11")
+        nc.sync.dma_start(out=m_raw[1, 1][:, :, 0:1024], in_=m_view[1, :, :, 1024:2048])
         nc.sync.dma_start(
             out=w_scales[64 : 68, :, :].bitcast(I32),
             in_=modes_scales[:, 8 : 12, :].rearrange("h r n -> r h n").bitcast(I32),
         )
+        nc.sync.dma_start(out=v_raw[3][:, 2:4, :], in_=v_view[3, :, 2:4, :])
         nc.sync.dma_start(
             out=w_scales[96 : 100, :, :].bitcast(I32),
             in_=modes_scales[:, 12 : 16, :].rearrange("h r n -> r h n").bitcast(I32),
         )
+        nc.sync.dma_start(out=w_words[:], in_=modes_words.rearrange("h p n -> p h n"))
 
         def codes(name, n):
             c = keep.tile([P, n], U32, name=name, align_bytes=64)
@@ -175,18 +171,16 @@ def tile_reynolds_stress_projection_s8_kernel(
                     nc.tensor.transpose(bank[:, at : at + P], words[:, lo : lo + P], ident[:])
 
         def broadcast():
-            nc.vector.tensor_copy(out=w8f[:], in_=w8[:])
-            for src, dst in ((w8f, w_b), (fs8, fs_b)):
-                for j in range(2):
-                    bank = bank_tile()
-                    for c in range(4):
-                        nc.tensor.transpose(
-                            bank[:, P * c : P * c + P], src[:, 4 * j + c : 4 * j + c + 1].to_broadcast([P, P]), ident[:]
-                        )
-                    nc.scalar.copy(
-                        out=dst[:].rearrange("p (w a j e) -> p j w a e", w=2, a=P, j=2)[:, j, :, :, :],
-                        in_=bank[:].rearrange("p (w e a) -> p w a e", w=2, e=2),
+            for j in range(2):
+                bank = bank_tile()
+                for c in range(4):
+                    nc.tensor.transpose(
+                        bank[:, P * c : P * c + P], fs8[:, 4 * j + c : 4 * j + c + 1].to_broadcast([P, P]), ident[:]
                     )
+                nc.scalar.copy(
+                    out=fs_b[:].rearrange("p (w a j e) -> p j w a e", w=2, a=P, j=2)[:, j, :, :, :],
+                    in_=bank[:].rearrange("p (w e a) -> p w a e", w=2, e=2),
+                )
 
         st = {}
 
@@ -198,10 +192,13 @@ def tile_reynolds_stress_projection_s8_kernel(
                 words_out(st["u", g, kk], b, bank, "s")
 
         def u_quant(g, b):
-            for kk in range(KK):
-                quantize(u_c[g, kk], st["u", g, kk], 256 * b, 256 * b + 256)
+            if g == 0:
+                for kk in range(KK):
+                    quantize(u_c[g, kk], st["u", g, kk], 256 * b, 256 * b + 256)
+            else:
+                quantize(u_c[g, b], st["u", g, b])
 
-        def v_turn0(h, kk):
+        def v_turn(h, kk):
             st["v", h, kk] = stage.tile([P, PASS, 4], BF16, name="v_st", align_bytes=64)
             for b in range(2):
                 bank = bank_tile()
@@ -213,31 +210,11 @@ def tile_reynolds_stress_projection_s8_kernel(
                     op=MULT,
                 )
 
-        v_m = {}
-
         def sorted_words(ap):
             return ap.rearrange("p (k w e) -> p w k e", w=2, e=2)
 
         def in_order(ap):
             return ap.rearrange("p (w k e) -> p w k e", w=2, e=2)
-
-        def v_mult(h, b):
-            if h not in v_m:
-                v_m[h] = stage.tile([P, Q, T], BF16, name="v_m")
-            for q in (2 * b, 2 * b + 1):
-                nc.vector.tensor_tensor(
-                    out=in_order(v_m[h][:, q, :]), in0=sorted_words(v_raw[h][:, q, :]), in1=in_order(w_b[:]), op=MULT
-                )
-
-        def v_turn(h, kk):
-            if h == 0:
-                v_turn0(h, kk)
-                return
-            st["v", h, kk] = stage.tile([P, PASS, 4], BF16, name="v_st", align_bytes=64)
-            for b in range(2):
-                bank = bank_tile()
-                turn_sorted(bank, v_m[h], b, kk)
-                words_out(st["v", h, kk], b, bank, "s")
 
         def v_quant(h, kk):
             quantize(v_c[h, kk], st["v", h, kk])
@@ -292,9 +269,13 @@ def tile_reynolds_stress_projection_s8_kernel(
         def f_scale(q):
             f_cast = stage.tile([P, X], BF16, name="f_cast")
             nc.scalar.copy(out=f_cast[:], in_=f_bytes[:, q, :].bitcast(FP8))
-            nc.gpsimd.tensor_tensor(
-                out=in_order(f_bf[:, q, :]), in0=sorted_words(f_cast[:]), in1=in_order(fs_b[:]), op=MULT
-            )
+            for w in range(2):
+                nc.gpsimd.tensor_tensor(
+                    out=in_order(f_bf[:, q, :])[:, w, :, :],
+                    in0=sorted_words(f_cast[:])[:, w, :, :],
+                    in1=in_order(fs_b[:])[:, w, :, :],
+                    op=MULT,
+                )
 
         def f_turn(g):
             st["f", g] = stage.tile([P, PASS, 4], BF16, name="u_st", align_bytes=64)
@@ -339,7 +320,7 @@ def tile_reynolds_stress_projection_s8_kernel(
             nc.sync.dma_start(out=coef_view[g, t], in_=o[:])
 
         units = {
-            "BT": broadcast, "UT": u_turn, "UQ": u_quant, "VM": v_mult, "VT": v_turn, "VQ": v_quant,
+            "BT": broadcast, "UT": u_turn, "UQ": u_quant, "VT": v_turn, "VQ": v_quant,
             "R": stress, "ST": s_turn, "SI": s_inter, "X": x_quant, "Y": y_quant,
             "F": f_scale, "FT": f_turn, "FQ": f_quant, "P": project_x, "C": project_y,
         }

@@ -3,8 +3,8 @@ from contextlib import ExitStack
 import concourse.mybir as mybir
 from concourse.masks import make_identity
 
-X, Y, T, D = 1024, 2048, 1024, 512
-FLOPS = 2 * X * Y * T + 4 * X * Y * D
+X, Y, K, D = 1024, 2048, 1024, 512
+FLOPS = 2 * X * Y * K + 2 * X * Y * D + 2 * D * X * Y
 
 F32 = mybir.dt.float32
 BF16 = mybir.dt.bfloat16
@@ -15,26 +15,14 @@ FP8 = mybir.dt.float8_e4m3fn
 FP8X4 = mybir.dt.float8_e4m3fn_x4
 FP4X4 = mybir.dt.float4_e2m1fn_x4
 MULT = mybir.AluOpType.mult
-SUB = mybir.AluOpType.subtract
+SUBTRACT = mybir.AluOpType.subtract
 
 P = 128
-PASS = 512
-G, H, KK = X // PASS, Y // PASS, T // PASS
-Q = 4
-
-PROGRAM = """
-BT VT01 VT00 VQ00 UT00 VQ01 UT01 UQ01 UT10 F3 UQ00 R003 R000 R002 R001 F1
-UQ10 UT11 VT10 UQ11 VT11 F2 ST001 VQ10 ST000 VQ11 R100 R101 F0 R102 R103 R011
-SI001 R012 R010 SI000 SI100 R013 SI101 R113 ST100 Y00 R110 FT0 X10 FT1 X00 FQ0
-ST010 ST011 SI011 VT20 SI010 FQ1 ST101 VQ20 VT21 Y01 R111 VQ21 P01 R112 P00 Y10
-VT31 SI111 R020 R021 R023 R022 VT30 VQ31 SI110 ST020 VQ30 X01 ST110 X11 ST111 ST021
-R122 R121 R120 SI021 R123 R132 SI020 R032 P11 R033 R031 SI121 R030 Y02 SI120 R130
-R133 P10 ST031 ST030 ST121 R131 ST120 ST131 ST130 SI131 Y03 Y11 X02 SI130 Y12 SI031
-SI030 C03 X12 C01 Y13 C02 C00 P20 C13 P21 X13 X03 C12 P31 P30 C10
-C11
-"""
-ON_V_X = ((2, 0), (2, 1), (3, 0), (3, 2), (3, 3))
-ON_V_Y = ((0, 0), (0, 1), (0, 2), (0, 3), (1, 2))
+PACK = 4
+GROUP = P * PACK
+PAIR = 2 * P
+XG, YG, KG = X // GROUP, Y // GROUP, K // GROUP
+SCALE_ROWS = 4
 
 
 def tile_reynolds_stress_projection_s8_kernel(
@@ -43,292 +31,328 @@ def tile_reynolds_stress_projection_s8_kernel(
     nc = tc.nc
     with ExitStack() as ctx:
         keep = ctx.enter_context(tc.tile_pool(name="keep", bufs=1))
-        raw = ctx.enter_context(tc.tile_pool(name="raw", bufs=4))
+        rows = ctx.enter_context(tc.tile_pool(name="rows", bufs=4))
         stage = ctx.enter_context(tc.tile_pool(name="stage", bufs=2))
-        outs = ctx.enter_context(tc.tile_pool(name="outs", bufs=4))
+        outs = ctx.enter_context(tc.tile_pool(name="outs", bufs=8))
         psum = ctx.enter_context(tc.psum_pool(name="psum", bufs=8))
-
-        def bank_tile():
-            bank = psum.tile([P, 512], F32, name="bank")
-            return bank
 
         ident = keep.tile([P, P], F32, name="ident")
         make_identity(nc, ident[:])
-        w_scales = keep.tile([P, H, D], U8, name="w_scales", align_bytes=64)
-        nc.gpsimd.memset(w_scales[:].rearrange("p h n -> p (h n)").bitcast(I32), 0)
 
-        w4 = keep.tile([P, KK, 2, 2], BF16, name="w4")
-        fs8 = keep.tile([P, 8], F32, name="fs8")
-        rho4 = keep.tile([P, G, Q], BF16, name="rho4")
-        fs_b = keep.tile([P, X], F32, name="fs_b")
-        u_raw, v_raw, m_raw = {}, {}, {}
-        u_view = u.rearrange("(g p t) k -> g p t k", p=P, t=Q)
-        v_view = v.rearrange("(h p q) k -> h p q k", p=P, q=Q)
-        m_view = model.rearrange("(g p t) y -> g p t y", p=P, t=Q)
+        u_view = u.rearrange("(g p j) k -> g p j k", p=P, j=PACK)
+        v_view = v.rearrange("(h p j) k -> h p j k", p=P, j=PACK)
+        model_view = model.rearrange("(g p j) y -> g p j y", p=P, j=PACK)
 
-        w_words = keep.tile([P, H, 2 * D], U8, name="w_words", align_bytes=64)
-        nc.sync.dma_start(out=fs8[:], in_=filt_scale.rearrange("o (p c) -> p (o c)", c=8))
-        nc.sync.dma_start(out=w4[:].rearrange("p g a b -> p g (a b)"), in_=weight.rearrange("(g p t) -> p g t", p=P, t=Q))
-        v_raw[0] = raw.tile([P, Q, T], BF16, name="rows")
-        nc.sync.dma_start(out=v_raw[0][:, 0:1, :], in_=v_view[0, :, 0:1, :])
-        nc.sync.dma_start(out=v_raw[0][:, 1:2, :], in_=v_view[0, :, 1:2, :])
-        nc.sync.dma_start(out=v_raw[0][:, 2:3, :], in_=v_view[0, :, 2:3, :])
-        nc.sync.dma_start(out=v_raw[0][:, 3:4, :], in_=v_view[0, :, 3:4, :])
-        u_raw[0] = raw.tile([P, Q, T], BF16, name="rows")
-        nc.sync.dma_start(out=u_raw[0][:, 0:1, :], in_=u_view[0, :, 0:1, :])
-        nc.sync.dma_start(out=u_raw[0][:, 1:2, :], in_=u_view[0, :, 1:2, :])
-        nc.sync.dma_start(out=u_raw[0][:, 2:3, :], in_=u_view[0, :, 2:3, :])
-        nc.sync.dma_start(out=u_raw[0][:, 3:4, :], in_=u_view[0, :, 3:4, :])
-        u_raw[1] = raw.tile([P, Q, T], BF16, name="rows")
-        nc.sync.dma_start(out=u_raw[1][:, 0:2, :], in_=u_view[1, :, 0:2, :])
-        nc.sync.dma_start(out=u_raw[1][:, 2:4, :], in_=u_view[1, :, 2:4, :])
-        m_raw[0, 0] = keep.tile([P, Q, Y // 2], BF16, name="m_raw00")
-        nc.sync.dma_start(out=m_raw[0, 0][:, :, 0:512], in_=m_view[0, :, :, 0:512])
-        f_bytes = keep.tile([P, Q, X], U8, name="f_bytes")
-        nc.sync.dma_start(out=f_bytes[:], in_=filt_bytes.rearrange("(p q) k -> p q k", q=Q))
-        v_raw[1] = raw.tile([P, Q, T], BF16, name="rows")
-        nc.sync.dma_start(out=v_raw[1][:, 0:2, :], in_=v_view[1, :, 0:2, :])
-        nc.sync.dma_start(out=v_raw[1][:, 2:4, :], in_=v_view[1, :, 2:4, :])
-        nc.sync.dma_start(out=rho4[:], in_=rho.rearrange("(g p t) -> p g t", p=P, t=Q))
-        v_raw[2] = raw.tile([P, Q, T], BF16, name="rows")
-        nc.sync.dma_start(out=v_raw[2][:, 0:2, :], in_=v_view[2, :, 0:2, :])
-        m_raw[1, 0] = keep.tile([P, Q, Y // 2], BF16, name="m_raw10")
-        nc.sync.dma_start(out=m_raw[1, 0][:, :, 0:1024], in_=m_view[1, :, :, 0:1024])
+        def load_rows(view, group, pieces):
+            tile = rows.tile([P, PACK, K], BF16, name="rows")
+            step = PACK // pieces
+            for j in range(0, PACK, step):
+                nc.sync.dma_start(out=tile[:, j : j + step, :], in_=view[group, :, j : j + step, :])
+            return tile
+
+        def load_model(g, h, width):
+            tile = keep.tile([P, PACK, width * GROUP], BF16, name=f"model_{g}{h}")
+            nc.sync.dma_start(out=tile[:], in_=model_view[g, :, :, h * GROUP : (h + width) * GROUP])
+            for i in range(width):
+                model_sb[g, h + i] = tile[:, :, i * GROUP : (i + 1) * GROUP]
+
+        u_rows, v_rows, model_sb = {}, {}, {}
+        fs_cols = keep.tile([P, 8], F32, name="fs_cols")
+        nc.sync.dma_start(out=fs_cols[:], in_=filt_scale.rearrange("o (p c) -> p (o c)", c=8))
+        weight_sb = keep.tile([P, KG, 2, 2], BF16, name="weight_sb")
         nc.sync.dma_start(
-            out=w_scales[0 : 4, :, :].bitcast(I32),
-            in_=modes_scales[:, 0 : 4, :].rearrange("h r n -> r h n").bitcast(I32),
+            out=weight_sb[:].rearrange("p n w e -> p n (w e)"),
+            in_=weight.rearrange("(n p j) -> p n j", p=P, j=PACK),
         )
-        nc.sync.dma_start(
-            out=w_scales[32 : 36, :, :].bitcast(I32),
-            in_=modes_scales[:, 4 : 8, :].rearrange("h r n -> r h n").bitcast(I32),
-        )
-        nc.sync.dma_start(out=m_raw[0, 0][:, :, 512:1024], in_=m_view[0, :, :, 512:1024])
-        m_raw[0, 1] = keep.tile([P, Q, Y // 2], BF16, name="m_raw01")
-        nc.sync.dma_start(out=m_raw[0, 1][:, :, 0:1024], in_=m_view[0, :, :, 1024:2048])
-        v_raw[3] = raw.tile([P, Q, T], BF16, name="rows")
-        nc.sync.dma_start(out=v_raw[3][:, 0:2, :], in_=v_view[3, :, 0:2, :])
-        nc.sync.dma_start(out=v_raw[2][:, 2:4, :], in_=v_view[2, :, 2:4, :])
-        m_raw[1, 1] = keep.tile([P, Q, Y // 2], BF16, name="m_raw11")
-        nc.sync.dma_start(out=m_raw[1, 1][:, :, 0:1024], in_=m_view[1, :, :, 1024:2048])
-        nc.sync.dma_start(
-            out=w_scales[64 : 68, :, :].bitcast(I32),
-            in_=modes_scales[:, 8 : 12, :].rearrange("h r n -> r h n").bitcast(I32),
-        )
-        nc.sync.dma_start(out=v_raw[3][:, 2:4, :], in_=v_view[3, :, 2:4, :])
-        nc.sync.dma_start(
-            out=w_scales[96 : 100, :, :].bitcast(I32),
-            in_=modes_scales[:, 12 : 16, :].rearrange("h r n -> r h n").bitcast(I32),
-        )
+        rho_sb = keep.tile([P, XG, PACK], BF16, name="rho_sb")
+        nc.sync.dma_start(out=rho_sb[:], in_=rho.rearrange("(g p j) -> p g j", p=P, j=PACK))
+        v_rows[0] = load_rows(v_view, 0, 4)
+        u_rows[0] = load_rows(u_view, 0, 4)
+        u_rows[1] = load_rows(u_view, 1, 2)
+        load_model(0, 0, 1)
+        filt_codes = keep.tile([P, PACK, X], U8, name="filt_codes")
+        nc.sync.dma_start(out=filt_codes[:], in_=filt_bytes.rearrange("(p j) x -> p j x", j=PACK))
+        v_rows[1] = load_rows(v_view, 1, 2)
+        load_model(1, 0, 2)
+        load_model(0, 1, 1)
+        v_rows[2] = load_rows(v_view, 2, 2)
+        v_rows[3] = load_rows(v_view, 3, 2)
+        load_model(0, 2, 2)
+        load_model(1, 2, 2)
+        w_words = keep.tile([P, YG, 2 * D], U8, name="w_words", align_bytes=64)
         nc.sync.dma_start(out=w_words[:], in_=modes_words.rearrange("h p n -> p h n"))
+        w_scales = keep.tile([P, YG, D], U8, name="w_scales", align_bytes=64)
+        nc.gpsimd.memset(w_scales[:].rearrange("p h n -> p (h n)").bitcast(I32), 0)
+        for q in range(4):
+            nc.sync.dma_start(
+                out=w_scales[32 * q : 32 * q + SCALE_ROWS, :, :].bitcast(I32),
+                in_=modes_scales[:, SCALE_ROWS * q : SCALE_ROWS * (q + 1), :].rearrange("h r n -> r h n").bitcast(I32),
+            )
 
-        def codes(name, n):
-            c = keep.tile([P, n], U32, name=name, align_bytes=64)
-            s = keep.tile([P, n], U8, name=name + "_s", align_bytes=64)
-            return c, s
+        def operand(name):
+            codes = keep.tile([P, GROUP], U32, name=name, align_bytes=64)
+            scales = keep.tile([P, GROUP], U8, name=name + "_scales", align_bytes=64)
+            return codes, scales
 
-        u_c = {(g, kk): codes(f"u_c{g}{kk}", PASS) for g in range(G) for kk in range(KK)}
-        v_c = {(h, kk): codes(f"v_c{h}{kk}", PASS) for h in range(H) for kk in range(KK)}
-        f_c = {g: codes(f"f_c{g}", D) for g in range(G)}
-        x_c = {(g, h): codes(f"x_c{g}{h}", PASS) for g in range(G) for h in range(H)}
-        y_c = {(g, h): codes(f"y_c{g}{h}", PASS) for g in range(G) for h in range(H)}
+        u_mx = {(g, n): operand(f"u_mx{g}{n}") for g in range(XG) for n in range(KG)}
+        v_mx = {(h, n): operand(f"v_mx{h}{n}") for h in range(YG) for n in range(KG)}
+        filt_mx = {g: operand(f"filt_mx{g}") for g in range(XG)}
+        sx_mx = {(g, h): operand(f"sx_mx{g}{h}") for g in range(XG) for h in range(YG)}
+        sy_mx = {(g, h): operand(f"sy_mx{g}{h}") for g in range(XG) for h in range(YG)}
 
-        def quantize(dst, src, lo=0, hi=PASS):
+        def quantize(dst, src, lo=0, hi=GROUP):
+            codes, scales = dst
             nc.vector.quantize_mx(
-                out=dst[0][:, lo:hi].bitcast(FP8X4),
-                scales=dst[1][:, lo:hi],
-                in_=src[:].rearrange("p n j -> p (n j)")[:, 4 * lo : 4 * hi],
+                out=codes[:, lo:hi].bitcast(FP8X4),
+                scales=scales[:, lo:hi],
+                in_=src[:, lo:hi, :].rearrange("p n j -> p (n j)"),
             )
 
-        def mx(out, a, a_cols, b, b_cols, start, stop):
-            nc.tensor.matmul_mx(
-                out=out, lhsT=a[0][:, a_cols].bitcast(FP8X4), lhsT_scale=a[1][:, a_cols],
-                rhs=b[0][:, b_cols].bitcast(FP8X4), rhs_scale=b[1][:, b_cols], start=start, stop=stop,
+        def packed_tile(name, bufs=2):
+            tile = stage.tile([P, GROUP, PACK], BF16, name=name, align_bytes=64, bufs=bufs)
+            return tile
+
+        def new_bank():
+            bank = psum.tile([P, GROUP], F32, name="bank")
+            return bank
+
+        def transpose_pair(word_slices):
+            bank = new_bank()
+            for w in range(2):
+                for i in range(2):
+                    at = PAIR * w + P * i
+                    nc.tensor.transpose(bank[:, at : at + P], word_slices[w][i], ident[:])
+            return bank
+
+        def strided_words(src, b, n):
+            lo, hi = n * PAIR, (n + 1) * PAIR
+            return [[src[:, 2 * b + i, :].bitcast(F32)[:, lo + w : hi : 2] for i in range(2)] for w in range(2)]
+
+        def sorted_words(src, b, n, groups):
+            views = [src[:, 2 * b + i, :].bitcast(F32) for i in range(2)]
+            starts = [P * (groups * w + n) for w in range(2)]
+            return [[view[:, s : s + P] for view in views] for s in starts]
+
+        def words_out(dst, b, bank):
+            cols = dst[:, PAIR * b : PAIR * (b + 1), :].rearrange("p r j -> p (r j)").bitcast(F32)
+            nc.scalar.copy(
+                out=cols.rearrange("p (r w) -> p r w", w=2), in_=bank[:].rearrange("p (w r) -> p r w", w=2)
             )
 
-        def copy_out(eng, out, in_):
-            if eng == "v":
-                nc.vector.tensor_copy(out=out, in_=in_)
-            else:
-                nc.scalar.copy(out=out, in_=in_)
+        u_packed, v_packed = {}, {}
 
-        def words_out(dst, b, bank, eng):
-            o = dst[:, 256 * b : 256 * b + 256, :].rearrange("p r j -> p (r j)").bitcast(F32).rearrange("p (r w) -> p r w", w=2)
-            copy_out(eng, o, bank[:].rearrange("p (w r) -> p r w", w=2))
+        def turn_u(g, n):
+            u_packed[g, n] = packed_tile("u_packed")
+            for b in range(2):
+                words_out(u_packed[g, n], b, transpose_pair(strided_words(u_rows[g], b, n)))
 
-        def turn(bank, src, b, kk):
-            for w in range(2):
-                for e in range(2):
-                    words = src[:, 2 * b + e, :].bitcast(F32)
-                    at = 256 * w + 128 * e
-                    nc.tensor.transpose(bank[:, at : at + P], words[:, 256 * kk + w : 256 * kk + 256 : 2], ident[:])
+        def turn_v(h, n):
+            v_packed[h, n] = packed_tile("v_packed")
+            for b in range(2):
+                bank = transpose_pair(strided_words(v_rows[h], b, n))
+                nc.vector.tensor_tensor(
+                    out=v_packed[h, n][:, PAIR * b : PAIR * (b + 1), :].rearrange("p r (w e) -> p r w e", w=2),
+                    in0=bank[:].bitcast(BF16).rearrange("p (w r e) -> p r w e", w=2, e=2),
+                    in1=weight_sb[:, n : n + 1, :, :].to_broadcast([P, PAIR, 2, 2]),
+                    op=MULT,
+                )
 
-        def turn_sorted(bank, src, b, kk):
-            for w in range(2):
-                for e in range(2):
-                    words = src[:, 2 * b + e, :].bitcast(F32)
-                    at = 256 * w + 128 * e
-                    lo = 256 * w + 128 * kk
-                    nc.tensor.transpose(bank[:, at : at + P], words[:, lo : lo + P], ident[:])
+        filt_scales = keep.tile([P, X], F32, name="filt_scales")
+        filt_bf = keep.tile([P, PACK, X], BF16, name="filt_bf")
+        filt_packed = {}
 
-        def broadcast():
-            for j in range(2):
-                bank = bank_tile()
+        def by_word_plain(ap):
+            return ap.rearrange("p (m w e) -> p w m e", w=2, e=2)
+
+        def by_word_sorted(ap):
+            return ap.rearrange("p (w m e) -> p w m e", w=2, e=2)
+
+        def spread_filt_scale():
+            for half in range(2):
+                bank = new_bank()
                 for c in range(4):
-                    nc.tensor.transpose(
-                        bank[:, P * c : P * c + P], fs8[:, 4 * j + c : 4 * j + c + 1].to_broadcast([P, P]), ident[:]
-                    )
+                    col = fs_cols[:, 4 * half + c : 4 * half + c + 1]
+                    nc.tensor.transpose(bank[:, P * c : P * (c + 1)], col.to_broadcast([P, P]), ident[:])
                 nc.scalar.copy(
-                    out=fs_b[:].rearrange("p (w a j e) -> p j w a e", w=2, a=P, j=2)[:, j, :, :, :],
+                    out=filt_scales[:].rearrange("p (w a half e) -> p half w a e", w=2, a=P, half=2)[:, half, :, :, :],
                     in_=bank[:].rearrange("p (w e a) -> p w a e", w=2, e=2),
                 )
 
-        st = {}
-
-        def u_turn(g, kk):
-            st["u", g, kk] = stage.tile([P, PASS, 4], BF16, name="u_st", align_bytes=64)
-            for b in range(2):
-                bank = bank_tile()
-                turn(bank, u_raw[g], b, kk)
-                words_out(st["u", g, kk], b, bank, "s")
-
-        def u_quant(g, b):
-            if g == 0:
-                for kk in range(KK):
-                    quantize(u_c[g, kk], st["u", g, kk], 256 * b, 256 * b + 256)
-            else:
-                quantize(u_c[g, b], st["u", g, b])
-
-        def v_turn(h, kk):
-            st["v", h, kk] = stage.tile([P, PASS, 4], BF16, name="v_st", align_bytes=64)
-            for b in range(2):
-                bank = bank_tile()
-                turn(bank, v_raw[h], b, kk)
-                nc.vector.tensor_tensor(
-                    out=st["v", h, kk][:, 256 * b : 256 * b + 256, :].rearrange("p r (w e) -> p r w e", w=2),
-                    in0=bank[:].bitcast(BF16).rearrange("p (w r e) -> p r w e", w=2, e=2),
-                    in1=w4[:, kk : kk + 1, :, :].to_broadcast([P, 256, 2, 2]),
-                    op=MULT,
-                )
-
-        def sorted_words(ap):
-            return ap.rearrange("p (k w e) -> p w k e", w=2, e=2)
-
-        def in_order(ap):
-            return ap.rearrange("p (w k e) -> p w k e", w=2, e=2)
-
-        def v_quant(h, kk):
-            quantize(v_c[h, kk], st["v", h, kk])
-
-        s_t, x_st, y_st = {}, {}, {}
-
-        def stress(g, h, t):
-            if (g, h) not in s_t:
-                s_t[g, h] = stage.tile([P, Q, PASS], BF16, name="s_t", align_bytes=64, bufs=3)
-            bank = bank_tile()
-            for kk in range(KK):
-                mx(bank[:], u_c[g, kk], slice(P * t, P * t + P), v_c[h, kk], slice(0, PASS), kk == 0, kk == KK - 1)
-            m = m_raw[g, h // 2][:, t, PASS * (h % 2) : PASS * (h % 2) + PASS]
-            for w in range(2):
-                nc.vector.scalar_tensor_tensor(
-                    out=s_t[g, h][:, t, 256 * w : 256 * w + 256].rearrange("p (c e) -> p c e", e=2),
-                    in0=bank[:, 256 * w : 256 * w + 256].rearrange("p (e c) -> p c e", e=2),
-                    scalar=rho4[:, g, t : t + 1],
-                    in1=m.rearrange("p (c w e) -> p w c e", w=2, e=2)[:, w, :, :],
-                    op0=MULT,
-                    op1=SUB,
-                )
-
-        def s_turn(g, h, b):
-            if (g, h) not in y_st:
-                y_st[g, h] = stage.tile([P, PASS, 4], BF16, name="y_st", align_bytes=64)
-            bank = bank_tile()
-            for w in range(2):
-                for e in range(2):
-                    words = s_t[g, h][:, 2 * b + e, :].bitcast(F32)
-                    at = 256 * w + 128 * e
-                    nc.tensor.transpose(bank[:, at : at + P], words[:, P * w : P * w + P], ident[:])
-            words_out(y_st[g, h], b, bank, "s")
-
-        def s_inter(g, h, half):
-            if (g, h) not in x_st:
-                x_st[g, h] = stage.tile([P, PASS, Q], BF16, name="x_st", align_bytes=64)
-            n = slice(256 * half, 256 * half + 256)
-            nc.scalar.copy(
-                out=x_st[g, h][:, n, :].rearrange("p (c i) t -> p c t i", i=4),
-                in_=s_t[g, h][:, :, n].rearrange("p t (c i) -> p c t i", i=4),
-            )
-
-        def x_quant(g, h):
-            quantize(x_c[g, h], x_st[g, h])
-
-        def y_quant(g, h):
-            quantize(y_c[g, h], y_st[g, h])
-
-        f_bf = keep.tile([P, Q, X], BF16, name="f_bf")
-
-        def f_scale(q):
-            f_cast = stage.tile([P, X], BF16, name="f_cast")
-            nc.scalar.copy(out=f_cast[:], in_=f_bytes[:, q, :].bitcast(FP8))
+        def scale_filt(j):
+            widened = stage.tile([P, X], BF16, name="widened", bufs=4)
+            nc.scalar.copy(out=widened[:], in_=filt_codes[:, j, :].bitcast(FP8))
             for w in range(2):
                 nc.gpsimd.tensor_tensor(
-                    out=in_order(f_bf[:, q, :])[:, w, :, :],
-                    in0=sorted_words(f_cast[:])[:, w, :, :],
-                    in1=in_order(fs_b[:])[:, w, :, :],
+                    out=by_word_sorted(filt_bf[:, j, :])[:, w, :, :],
+                    in0=by_word_plain(widened[:])[:, w, :, :],
+                    in1=by_word_sorted(filt_scales[:])[:, w, :, :],
                     op=MULT,
                 )
 
-        def f_turn(g):
-            st["f", g] = stage.tile([P, PASS, 4], BF16, name="u_st", align_bytes=64)
+        def turn_filt(g):
+            filt_packed[g] = packed_tile("u_packed")
             for b in range(2):
-                bank = bank_tile()
-                turn_sorted(bank, f_bf, b, g)
-                words_out(st["f", g], b, bank, "s")
+                words_out(filt_packed[g], b, transpose_pair(sorted_words(filt_bf, b, g, XG)))
 
-        def f_quant(g):
-            quantize(f_c[g], st["f", g])
+        s_sb, sx_packed, sy_packed = {}, {}, {}
 
-        resp_view = resp.rearrange("(m q) y -> q m y", q=Q)
-        coef_view = coef.rearrange("(g m t) d -> g t m d", m=P, t=Q)
-
-        def project_x(h, b):
-            for q in (2 * b, 2 * b + 1):
-                bank = bank_tile()
-                for g in range(G):
-                    mx(bank[:], f_c[g], slice(P * q, P * q + P), x_c[g, h], slice(0, PASS), g == 0, g == G - 1)
-                o = outs.tile([P, PASS], F32, name="o_sb")
-                copy_out(
-                    "v" if (h, q) in ON_V_X else "s",
-                    o[:].rearrange("p (c w e) -> p c w e", w=2, e=2),
-                    bank[:].rearrange("p (w c e) -> p c w e", w=2, e=2),
-                )
-                nc.sync.dma_start(out=resp_view[q, :, PASS * h : PASS * h + PASS], in_=o[:])
-
-        def project_y(g, t):
-            bank = bank_tile()
-            for h in range(H):
+        def stress(g, h, j):
+            if j == 0:
+                s_sb[g, h] = stage.tile([P, PACK, GROUP], BF16, name="s_sb", align_bytes=64, bufs=3)
+            bank = new_bank()
+            for n in range(KG):
+                u_codes, u_scales = u_mx[g, n]
+                v_codes, v_scales = v_mx[h, n]
                 nc.tensor.matmul_mx(
                     out=bank[:],
-                    lhsT=y_c[g, h][0][:, P * t : P * t + P].bitcast(FP8X4),
-                    lhsT_scale=y_c[g, h][1][:, P * t : P * t + P],
+                    lhsT=u_codes[:, P * j : P * (j + 1)].bitcast(FP8X4),
+                    lhsT_scale=u_scales[:, P * j : P * (j + 1)],
+                    rhs=v_codes[:].bitcast(FP8X4),
+                    rhs_scale=v_scales[:],
+                    start=n == 0,
+                    stop=n == KG - 1,
+                )
+            for w in range(2):
+                cols = slice(PAIR * w, PAIR * (w + 1))
+                nc.vector.scalar_tensor_tensor(
+                    out=s_sb[g, h][:, j, cols].rearrange("p (m e) -> p m e", e=2),
+                    in0=bank[:, cols].rearrange("p (e m) -> p m e", e=2),
+                    scalar=rho_sb[:, g, j : j + 1],
+                    in1=model_sb[g, h][:, j, :].rearrange("p (m w e) -> p w m e", w=2, e=2)[:, w, :, :],
+                    op0=MULT,
+                    op1=SUBTRACT,
+                )
+
+        def turn_s(g, h):
+            sy_packed[g, h] = packed_tile("sy_packed", bufs=3)
+            for b in range(2):
+                words_out(sy_packed[g, h], b, transpose_pair(sorted_words(s_sb[g, h], b, 0, 1)))
+
+        def interleave_s(g, h):
+            sx_packed[g, h] = packed_tile("sx_packed")
+            for half in range(2):
+                cols = slice(PAIR * half, PAIR * (half + 1))
+                nc.scalar.copy(
+                    out=sx_packed[g, h][:, cols, :].rearrange("p (c i) j -> p c j i", i=4),
+                    in_=s_sb[g, h][:, :, cols].rearrange("p j (c i) -> p c j i", i=4),
+                )
+
+        coef_view = coef.rearrange("(g p j) d -> g j p d", p=P, j=PACK)
+        resp_view = resp.rearrange("(p j) y -> j p y", j=PACK)
+
+        def project_y(g, j):
+            bank = new_bank()
+            for h in range(YG):
+                codes, scales = sy_mx[g, h]
+                nc.tensor.matmul_mx(
+                    out=bank[:],
+                    lhsT=codes[:, P * j : P * (j + 1)].bitcast(FP8X4),
+                    lhsT_scale=scales[:, P * j : P * (j + 1)],
                     rhs=w_words[:, h, :].bitcast(FP4X4),
                     rhs_scale=w_scales[:, h, :],
                     start=h == 0,
-                    stop=h == H - 1,
+                    stop=h == YG - 1,
                 )
-            o = outs.tile([P, D], F32, name="o_sb")
-            copy_out("v" if (g, t) in ON_V_Y else "s", o[:], bank[:])
-            nc.sync.dma_start(out=coef_view[g, t], in_=o[:])
+            out = outs.tile([P, D], F32, name="out")
+            if j % 2:
+                nc.vector.tensor_copy(out=out[:], in_=bank[:])
+            else:
+                nc.scalar.copy(out=out[:], in_=bank[:])
+            nc.sync.dma_start(out=coef_view[g, j], in_=out[:])
 
-        units = {
-            "BT": broadcast, "UT": u_turn, "UQ": u_quant, "VT": v_turn, "VQ": v_quant,
-            "R": stress, "ST": s_turn, "SI": s_inter, "X": x_quant, "Y": y_quant,
-            "F": f_scale, "FT": f_turn, "FQ": f_quant, "P": project_x, "C": project_y,
-        }
+        def project_x(h, j):
+            bank = new_bank()
+            for g in range(XG):
+                f_codes, f_scales = filt_mx[g]
+                s_codes, s_scales = sx_mx[g, h]
+                nc.tensor.matmul_mx(
+                    out=bank[:],
+                    lhsT=f_codes[:, P * j : P * (j + 1)].bitcast(FP8X4),
+                    lhsT_scale=f_scales[:, P * j : P * (j + 1)],
+                    rhs=s_codes[:].bitcast(FP8X4),
+                    rhs_scale=s_scales[:],
+                    start=g == 0,
+                    stop=g == XG - 1,
+                )
+            out = outs.tile([P, GROUP], F32, name="out")
+            nc.scalar.copy(
+                out=out[:].rearrange("p (m w e) -> p m w e", w=2, e=2),
+                in_=bank[:].rearrange("p (w m e) -> p m w e", w=2, e=2),
+            )
+            nc.sync.dma_start(out=resp_view[j, :, h * GROUP : (h + 1) * GROUP], in_=out[:])
+
         with tc.manual_schedule():
-            for word in PROGRAM.split():
-                n = len(word)
-                cut = n
-                for i in range(n):
-                    if word[i] in "01234567" and cut == n:
-                        cut = i
-                units[word[:cut]](*[int(c) for c in word[cut:]])
+            spread_filt_scale()
+            for n in range(KG):
+                turn_v(0, n)
+            for n in range(KG):
+                quantize(v_mx[0, n], v_packed[0, n])
+            for g in range(XG):
+                for n in range(KG):
+                    turn_u(g, n)
+            for half in range(2):
+                for n in range(KG):
+                    quantize(u_mx[0, n], u_packed[0, n], PAIR * half, PAIR * (half + 1))
+            scale_filt(0)
+            scale_filt(1)
+            for n in range(KG):
+                quantize(u_mx[1, n], u_packed[1, n])
+            for j in range(PACK):
+                stress(0, 0, j)
+            for n in range(KG):
+                turn_v(1, n)
+            turn_s(0, 0)
+            scale_filt(2)
+            scale_filt(3)
+            interleave_s(0, 0)
+            for n in range(KG):
+                quantize(v_mx[1, n], v_packed[1, n])
+
+            for h in range(YG):
+                if h == 1:
+                    for g in range(XG):
+                        quantize(filt_mx[g], filt_packed[g])
+                stress(1, h, 0)
+                if h > 0:
+                    quantize(sx_mx[1, h - 1], sx_packed[1, h - 1])
+                for j in range(1, PACK):
+                    stress(1, h, j)
+                if h + 1 < YG:
+                    for j in range(PACK):
+                        stress(0, h + 1, j)
+                if h > 0:
+                    for j in range(0, PACK // 2):
+                        project_x(h - 1, j)
+                quantize(sy_mx[0, h], sy_packed[0, h])
+                if h > 0:
+                    quantize(sy_mx[1, h - 1], sy_packed[1, h - 1])
+                turn_s(1, h)
+                interleave_s(1, h)
+                if h > 0:
+                    for j in range(PACK // 2, PACK):
+                        project_x(h - 1, j)
+                if h + 2 < YG:
+                    for n in range(KG):
+                        turn_v(h + 2, n)
+                if h == 0:
+                    for g in range(XG):
+                        turn_filt(g)
+                if h + 2 < YG:
+                    for n in range(KG):
+                        quantize(v_mx[h + 2, n], v_packed[h + 2, n])
+                if h + 1 < YG:
+                    turn_s(0, h + 1)
+                quantize(sx_mx[0, h], sx_packed[0, h])
+                if h + 1 < YG:
+                    interleave_s(0, h + 1)
+
+            last = YG - 1
+            quantize(sy_mx[1, last], sy_packed[1, last])
+            project_y(0, 0)
+            quantize(sx_mx[1, last], sx_packed[1, last])
+            for j in range(1, PACK):
+                project_y(0, j)
+            for j in range(PACK):
+                project_y(1, j)
+            for j in range(PACK):
+                project_x(last, j)

from contextlib import ExitStack

import concourse.mybir as mybir
from concourse.masks import make_identity

X, Y, K, D = 1024, 2048, 1024, 512
FLOPS = 2 * X * Y * K + 2 * X * Y * D + 2 * D * X * Y

F32 = mybir.dt.float32
BF16 = mybir.dt.bfloat16
I32 = mybir.dt.int32
U32 = mybir.dt.uint32
U8 = mybir.dt.uint8
FP8 = mybir.dt.float8_e4m3fn
FP8X4 = mybir.dt.float8_e4m3fn_x4
FP4X4 = mybir.dt.float4_e2m1fn_x4
MULT = mybir.AluOpType.mult
SUBTRACT = mybir.AluOpType.subtract

P = 128
PACK = 4
GROUP = P * PACK
PAIR = 2 * P
XG, YG, KG = X // GROUP, Y // GROUP, K // GROUP
SCALE_ROWS = 4


def tile_reynolds_stress_projection_s8_kernel(
    tc, u, v, weight, rho, model, modes_words, modes_scales, filt_bytes, filt_scale, coef, resp
):
    nc = tc.nc
    with ExitStack() as ctx:
        keep = ctx.enter_context(tc.tile_pool(name="keep", bufs=1))
        rows = ctx.enter_context(tc.tile_pool(name="rows", bufs=4))
        stage = ctx.enter_context(tc.tile_pool(name="stage", bufs=2))
        outs = ctx.enter_context(tc.tile_pool(name="outs", bufs=8))
        psum = ctx.enter_context(tc.psum_pool(name="psum", bufs=8))

        ident = keep.tile([P, P], F32, name="ident")
        make_identity(nc, ident[:])

        u_view = u.rearrange("(g p j) k -> g p j k", p=P, j=PACK)
        v_view = v.rearrange("(h p j) k -> h p j k", p=P, j=PACK)
        model_view = model.rearrange("(g p j) y -> g p j y", p=P, j=PACK)

        def load_rows(view, group, pieces):
            tile = rows.tile([P, PACK, K], BF16, name="rows")
            step = PACK // pieces
            for j in range(0, PACK, step):
                nc.sync.dma_start(out=tile[:, j : j + step, :], in_=view[group, :, j : j + step, :])
            return tile

        def load_model(g, h, width):
            tile = keep.tile([P, PACK, width * GROUP], BF16, name=f"model_{g}{h}")
            nc.sync.dma_start(out=tile[:], in_=model_view[g, :, :, h * GROUP : (h + width) * GROUP])
            for i in range(width):
                model_sb[g, h + i] = tile[:, :, i * GROUP : (i + 1) * GROUP]

        u_rows, v_rows, model_sb = {}, {}, {}
        fs_cols = keep.tile([P, 8], F32, name="fs_cols")
        nc.sync.dma_start(out=fs_cols[:], in_=filt_scale.rearrange("o (p c) -> p (o c)", c=8))
        weight_sb = keep.tile([P, KG, 2, 2], BF16, name="weight_sb")
        nc.sync.dma_start(
            out=weight_sb[:].rearrange("p n w e -> p n (w e)"),
            in_=weight.rearrange("(n p j) -> p n j", p=P, j=PACK),
        )
        rho_sb = keep.tile([P, XG, PACK], BF16, name="rho_sb")
        nc.sync.dma_start(out=rho_sb[:], in_=rho.rearrange("(g p j) -> p g j", p=P, j=PACK))
        v_rows[0] = load_rows(v_view, 0, 4)
        u_rows[0] = load_rows(u_view, 0, 4)
        u_rows[1] = load_rows(u_view, 1, 2)
        load_model(0, 0, 1)
        filt_codes = keep.tile([P, PACK, X], U8, name="filt_codes")
        nc.sync.dma_start(out=filt_codes[:], in_=filt_bytes.rearrange("(p j) x -> p j x", j=PACK))
        v_rows[1] = load_rows(v_view, 1, 2)
        load_model(1, 0, 2)
        load_model(0, 1, 1)
        v_rows[2] = load_rows(v_view, 2, 2)
        v_rows[3] = load_rows(v_view, 3, 2)
        load_model(0, 2, 2)
        load_model(1, 2, 2)
        w_words = keep.tile([P, YG, 2 * D], U8, name="w_words", align_bytes=64)
        nc.sync.dma_start(out=w_words[:], in_=modes_words.rearrange("h p n -> p h n"))
        w_scales = keep.tile([P, YG, D], U8, name="w_scales", align_bytes=64)
        nc.gpsimd.memset(w_scales[:].rearrange("p h n -> p (h n)").bitcast(I32), 0)
        for q in range(4):
            nc.sync.dma_start(
                out=w_scales[32 * q : 32 * q + SCALE_ROWS, :, :].bitcast(I32),
                in_=modes_scales[:, SCALE_ROWS * q : SCALE_ROWS * (q + 1), :].rearrange("h r n -> r h n").bitcast(I32),
            )

        def operand(name):
            codes = keep.tile([P, GROUP], U32, name=name, align_bytes=64)
            scales = keep.tile([P, GROUP], U8, name=name + "_scales", align_bytes=64)
            return codes, scales

        u_mx = {(g, n): operand(f"u_mx{g}{n}") for g in range(XG) for n in range(KG)}
        v_mx = {(h, n): operand(f"v_mx{h}{n}") for h in range(YG) for n in range(KG)}
        filt_mx = {g: operand(f"filt_mx{g}") for g in range(XG)}
        sx_mx = {(g, h): operand(f"sx_mx{g}{h}") for g in range(XG) for h in range(YG)}
        sy_mx = {(g, h): operand(f"sy_mx{g}{h}") for g in range(XG) for h in range(YG)}

        def quantize(dst, src, lo=0, hi=GROUP):
            codes, scales = dst
            nc.vector.quantize_mx(
                out=codes[:, lo:hi].bitcast(FP8X4),
                scales=scales[:, lo:hi],
                in_=src[:, lo:hi, :].rearrange("p n j -> p (n j)"),
            )

        def packed_tile(name, bufs=2):
            tile = stage.tile([P, GROUP, PACK], BF16, name=name, align_bytes=64, bufs=bufs)
            return tile

        def new_bank():
            bank = psum.tile([P, GROUP], F32, name="bank")
            return bank

        def transpose_pair(word_slices):
            bank = new_bank()
            for w in range(2):
                for i in range(2):
                    at = PAIR * w + P * i
                    nc.tensor.transpose(bank[:, at : at + P], word_slices[w][i], ident[:])
            return bank

        def strided_words(src, b, n):
            lo, hi = n * PAIR, (n + 1) * PAIR
            return [[src[:, 2 * b + i, :].bitcast(F32)[:, lo + w : hi : 2] for i in range(2)] for w in range(2)]

        def sorted_words(src, b, n, groups):
            views = [src[:, 2 * b + i, :].bitcast(F32) for i in range(2)]
            starts = [P * (groups * w + n) for w in range(2)]
            return [[view[:, s : s + P] for view in views] for s in starts]

        def words_out(dst, b, bank):
            cols = dst[:, PAIR * b : PAIR * (b + 1), :].rearrange("p r j -> p (r j)").bitcast(F32)
            nc.scalar.copy(
                out=cols.rearrange("p (r w) -> p r w", w=2), in_=bank[:].rearrange("p (w r) -> p r w", w=2)
            )

        u_packed, v_packed = {}, {}

        def turn_u(g, n):
            u_packed[g, n] = packed_tile("u_packed")
            for b in range(2):
                words_out(u_packed[g, n], b, transpose_pair(strided_words(u_rows[g], b, n)))

        def turn_v(h, n):
            v_packed[h, n] = packed_tile("v_packed")
            for b in range(2):
                bank = transpose_pair(strided_words(v_rows[h], b, n))
                nc.vector.tensor_tensor(
                    out=v_packed[h, n][:, PAIR * b : PAIR * (b + 1), :].rearrange("p r (w e) -> p r w e", w=2),
                    in0=bank[:].bitcast(BF16).rearrange("p (w r e) -> p r w e", w=2, e=2),
                    in1=weight_sb[:, n : n + 1, :, :].to_broadcast([P, PAIR, 2, 2]),
                    op=MULT,
                )

        filt_scales = keep.tile([P, X], F32, name="filt_scales")
        filt_bf = keep.tile([P, PACK, X], BF16, name="filt_bf")
        filt_packed = {}

        def by_word_plain(ap):
            return ap.rearrange("p (m w e) -> p w m e", w=2, e=2)

        def by_word_sorted(ap):
            return ap.rearrange("p (w m e) -> p w m e", w=2, e=2)

        def spread_filt_scale():
            for half in range(2):
                bank = new_bank()
                for c in range(4):
                    col = fs_cols[:, 4 * half + c : 4 * half + c + 1]
                    nc.tensor.transpose(bank[:, P * c : P * (c + 1)], col.to_broadcast([P, P]), ident[:])
                nc.scalar.copy(
                    out=filt_scales[:].rearrange("p (w a half e) -> p half w a e", w=2, a=P, half=2)[:, half, :, :, :],
                    in_=bank[:].rearrange("p (w e a) -> p w a e", w=2, e=2),
                )

        def scale_filt(j):
            widened = stage.tile([P, X], BF16, name="widened", bufs=4)
            nc.scalar.copy(out=widened[:], in_=filt_codes[:, j, :].bitcast(FP8))
            for w in range(2):
                nc.gpsimd.tensor_tensor(
                    out=by_word_sorted(filt_bf[:, j, :])[:, w, :, :],
                    in0=by_word_plain(widened[:])[:, w, :, :],
                    in1=by_word_sorted(filt_scales[:])[:, w, :, :],
                    op=MULT,
                )

        def turn_filt(g):
            filt_packed[g] = packed_tile("u_packed")
            for b in range(2):
                words_out(filt_packed[g], b, transpose_pair(sorted_words(filt_bf, b, g, XG)))

        s_sb, sx_packed, sy_packed = {}, {}, {}

        def stress(g, h, j):
            if j == 0:
                s_sb[g, h] = stage.tile([P, PACK, GROUP], BF16, name="s_sb", align_bytes=64, bufs=3)
            bank = new_bank()
            for n in range(KG):
                u_codes, u_scales = u_mx[g, n]
                v_codes, v_scales = v_mx[h, n]
                nc.tensor.matmul_mx(
                    out=bank[:],
                    lhsT=u_codes[:, P * j : P * (j + 1)].bitcast(FP8X4),
                    lhsT_scale=u_scales[:, P * j : P * (j + 1)],
                    rhs=v_codes[:].bitcast(FP8X4),
                    rhs_scale=v_scales[:],
                    start=n == 0,
                    stop=n == KG - 1,
                )
            for w in range(2):
                cols = slice(PAIR * w, PAIR * (w + 1))
                nc.vector.scalar_tensor_tensor(
                    out=s_sb[g, h][:, j, cols].rearrange("p (m e) -> p m e", e=2),
                    in0=bank[:, cols].rearrange("p (e m) -> p m e", e=2),
                    scalar=rho_sb[:, g, j : j + 1],
                    in1=model_sb[g, h][:, j, :].rearrange("p (m w e) -> p w m e", w=2, e=2)[:, w, :, :],
                    op0=MULT,
                    op1=SUBTRACT,
                )

        def turn_s(g, h):
            sy_packed[g, h] = packed_tile("sy_packed", bufs=3)
            for b in range(2):
                words_out(sy_packed[g, h], b, transpose_pair(sorted_words(s_sb[g, h], b, 0, 1)))

        def interleave_s(g, h):
            sx_packed[g, h] = packed_tile("sx_packed")
            for half in range(2):
                cols = slice(PAIR * half, PAIR * (half + 1))
                nc.scalar.copy(
                    out=sx_packed[g, h][:, cols, :].rearrange("p (c i) j -> p c j i", i=4),
                    in_=s_sb[g, h][:, :, cols].rearrange("p j (c i) -> p c j i", i=4),
                )

        coef_view = coef.rearrange("(g p j) d -> g j p d", p=P, j=PACK)
        resp_view = resp.rearrange("(p j) y -> j p y", j=PACK)

        def project_y(g, j):
            bank = new_bank()
            for h in range(YG):
                codes, scales = sy_mx[g, h]
                nc.tensor.matmul_mx(
                    out=bank[:],
                    lhsT=codes[:, P * j : P * (j + 1)].bitcast(FP8X4),
                    lhsT_scale=scales[:, P * j : P * (j + 1)],
                    rhs=w_words[:, h, :].bitcast(FP4X4),
                    rhs_scale=w_scales[:, h, :],
                    start=h == 0,
                    stop=h == YG - 1,
                )
            out = outs.tile([P, D], F32, name="out")
            if j % 2:
                nc.vector.tensor_copy(out=out[:], in_=bank[:])
            else:
                nc.scalar.copy(out=out[:], in_=bank[:])
            nc.sync.dma_start(out=coef_view[g, j], in_=out[:])

        def project_x(h, j):
            bank = new_bank()
            for g in range(XG):
                f_codes, f_scales = filt_mx[g]
                s_codes, s_scales = sx_mx[g, h]
                nc.tensor.matmul_mx(
                    out=bank[:],
                    lhsT=f_codes[:, P * j : P * (j + 1)].bitcast(FP8X4),
                    lhsT_scale=f_scales[:, P * j : P * (j + 1)],
                    rhs=s_codes[:].bitcast(FP8X4),
                    rhs_scale=s_scales[:],
                    start=g == 0,
                    stop=g == XG - 1,
                )
            out = outs.tile([P, GROUP], F32, name="out")
            nc.scalar.copy(
                out=out[:].rearrange("p (m w e) -> p m w e", w=2, e=2),
                in_=bank[:].rearrange("p (w m e) -> p m w e", w=2, e=2),
            )
            nc.sync.dma_start(out=resp_view[j, :, h * GROUP : (h + 1) * GROUP], in_=out[:])

        with tc.manual_schedule():
            spread_filt_scale()
            for n in range(KG):
                turn_v(0, n)
            for n in range(KG):
                quantize(v_mx[0, n], v_packed[0, n])
            for g in range(XG):
                for n in range(KG):
                    turn_u(g, n)
            for half in range(2):
                for n in range(KG):
                    quantize(u_mx[0, n], u_packed[0, n], PAIR * half, PAIR * (half + 1))
            scale_filt(0)
            scale_filt(1)
            for n in range(KG):
                quantize(u_mx[1, n], u_packed[1, n])
            for j in range(PACK):
                stress(0, 0, j)
            for n in range(KG):
                turn_v(1, n)
            turn_s(0, 0)
            scale_filt(2)
            scale_filt(3)
            interleave_s(0, 0)
            for n in range(KG):
                quantize(v_mx[1, n], v_packed[1, n])

            for h in range(YG):
                if h == 1:
                    for g in range(XG):
                        quantize(filt_mx[g], filt_packed[g])
                stress(1, h, 0)
                if h > 0:
                    quantize(sx_mx[1, h - 1], sx_packed[1, h - 1])
                for j in range(1, PACK):
                    stress(1, h, j)
                if h + 1 < YG:
                    for j in range(PACK):
                        stress(0, h + 1, j)
                if h > 0:
                    for j in range(0, PACK // 2):
                        project_x(h - 1, j)
                quantize(sy_mx[0, h], sy_packed[0, h])
                if h > 0:
                    quantize(sy_mx[1, h - 1], sy_packed[1, h - 1])
                turn_s(1, h)
                interleave_s(1, h)
                if h > 0:
                    for j in range(PACK // 2, PACK):
                        project_x(h - 1, j)
                if h + 2 < YG:
                    for n in range(KG):
                        turn_v(h + 2, n)
                if h == 0:
                    for g in range(XG):
                        turn_filt(g)
                if h + 2 < YG:
                    for n in range(KG):
                        quantize(v_mx[h + 2, n], v_packed[h + 2, n])
                if h + 1 < YG:
                    turn_s(0, h + 1)
                quantize(sx_mx[0, h], sx_packed[0, h])
                if h + 1 < YG:
                    interleave_s(0, h + 1)

            last = YG - 1
            quantize(sy_mx[1, last], sy_packed[1, last])
            project_y(0, 0)
            quantize(sx_mx[1, last], sx_packed[1, last])
            for j in range(1, PACK):
                project_y(0, j)
            for j in range(PACK):
                project_y(1, j)
            for j in range(PACK):
                project_x(last, j)
